import numpy as np, ml_dtypes
CORES = [24,48,72,152,176,200]
N = 6
TOK, K, FT = 512, 3, 1
ROUTE = [[[1,2,4],[1,3,5],[0,1,3],[1,4,5],[0,1,3],[0,1,3],[2,3,5],[1,2,3],[0,1,5],[1,2,3],[0,2,5],[1,3,4],[1,4,5],[0,2,5],[0,1,2],[3,4,5],[0,3,5],[2,3,4],[1,2,3],[1,2,3],[1,2,4],[2,3,4],[0,1,5],[1,4,5],[1,3,5],[0,1,3],[2,3,4],[2,4,5],[0,3,4],[1,3,5],[0,1,2],[0,3,5],[0,3,5],[0,2,3],[1,4,5],[0,3,5],[2,4,5],[1,3,4],[1,3,4],[0,1,4],[0,1,4],[0,3,4],[2,4,5],[2,3,4],[0,1,2],[1,2,5],[2,3,4],[3,4,5],[1,3,4],[0,1,5],[0,4,5],[0,1,5],[0,1,5],[0,3,4],[0,3,4],[1,2,5],[0,3,5],[0,1,3],[0,1,4],[0,3,4],[1,4,5],[0,2,3],[1,2,4],[0,1,5],[2,3,5],[0,2,3],[3,4,5],[0,3,5],[0,1,2],[0,1,4],[1,2,5],[0,1,4],[0,4,5],[2,3,5],[0,2,5],[0,1,2],[0,1,2],[1,2,5],[0,3,5],[1,2,4],[1,3,5],[1,3,5],[2,3,4],[2,3,5],[0,2,3],[1,2,3],[0,2,5],[0,1,3],[0,3,4],[1,4,5],[0,3,4],[0,3,4],[0,3,4],[1,2,5],[0,4,5],[0,2,3],[2,4,5],[2,3,5],[1,2,3],[0,1,5],[0,1,4],[0,2,3],[1,2,5],[2,3,4],[1,2,3],[0,1,5],[0,2,3],[1,2,3],[0,2,5],[0,1,3],[1,2,5],[1,3,4],[1,3,5],[1,2,3],[3,4,5],[0,2,5],[0,4,5],[0,1,5],[3,4,5],[0,1,4],[0,1,4],[3,4,5],[0,2,3],[1,3,4],[1,2,5],[1,4,5],[0,2,3],[0,2,3],[0,1,3],[0,3,5],[0,2,3],[0,3,4],[3,4,5],[0,1,2],[0,1,2],[0,1,2],[1,3,5],[1,2,5],[0,2,5],[0,3,5],[0,4,5],[2,3,5],[0,1,3],[1,2,4],[0,2,5],[1,2,5],[1,2,4],[0,1,4],[2,4,5],[2,3,4],[2,3,4],[1,2,5],[3,4,5],[0,4,5],[0,1,4],[0,3,4],[0,1,3],[1,2,5],[0,3,4],[0,3,5],[0,3,4],[2,3,5],[1,2,4],[0,2,3],[3,4,5],[1,3,5],[3,4,5],[2,4,5],[0,1,5],[0,2,3],[0,4,5],[1,2,4],[0,4,5],[0,1,4],[0,1,5],[0,2,3],[2,4,5],[0,2,4],[0,3,5],[2,3,4],[2,3,4],[3,4,5],[1,2,4],[0,1,4],[2,3,4],[0,3,5],[0,1,2],[1,3,4],[0,3,4],[2,4,5],[2,3,4],[0,2,5],[1,3,4],[0,1,5],[1,3,5],[0,1,5],[2,3,5],[0,1,2],[2,3,5],[2,3,5],[1,2,3],[0,2,5],[1,3,5],[0,1,4],[0,2,4],[2,4,5],[0,2,4],[0,1,5],[2,3,5],[3,4,5],[1,3,4],[1,2,5],[0,4,5],[0,3,4],[0,3,4],[0,2,5],[1,4,5],[2,4,5],[2,3,5],[0,1,5],[0,2,4],[0,3,4],[1,2,3],[0,1,3],[0,2,5],[0,2,5],[1,3,4],[0,2,4],[0,1,2],[0,3,4],[0,3,5],[0,1,5],[2,4,5],[0,4,5],[0,2,3],[0,1,5],[0,2,4],[0,2,3],[0,3,5],[0,3,5],[0,2,3],[3,4,5],[1,3,4],[3,4,5],[0,2,4],[0,2,5],[0,3,4],[3,4,5],[0,3,5],[1,3,4],[0,2,3],[1,2,4],[0,3,5],[0,3,5],[0,3,5],[0,2,5],[1,3,4],[0,2,3],[1,2,4],[0,4,5],[0,2,3],[0,3,5],[1,2,4],[0,1,3],[2,3,5],[1,3,5],[0,1,2],[2,4,5],[0,1,3],[2,4,5],[1,2,4],[2,3,4],[2,3,5],[1,2,4],[1,4,5],[0,1,4],[1,3,4],[3,4,5],[1,4,5],[2,4,5],[2,3,5],[2,4,5],[1,3,5],[0,4,5],[2,3,4],[1,2,3],[1,2,5],[0,4,5],[3,4,5],[0,1,5],[2,3,4],[1,2,5],[2,3,4],[3,4,5],[1,2,5],[1,2,4],[0,2,3],[1,4,5],[0,2,3],[0,3,4],[1,2,3],[1,3,4],[0,1,5],[0,1,5],[0,1,3],[1,3,4],[2,3,4],[1,2,3],[2,3,4],[0,4,5],[0,2,4],[0,1,4],[1,4,5],[1,2,5],[1,2,5],[0,2,5],[0,2,5],[0,1,3],[0,1,3],[2,4,5],[1,2,4],[0,1,4],[1,4,5],[0,2,4],[3,4,5],[0,2,5],[1,4,5],[1,3,5],[0,3,5],[1,2,3],[2,3,5],[1,3,4],[0,2,4],[1,2,3],[1,2,4],[0,2,4],[0,1,4],[2,3,4],[1,2,5],[1,2,5],[1,2,4],[1,2,3],[0,1,3],[0,2,5],[3,4,5],[1,3,5],[0,1,3],[1,3,5],[1,4,5],[0,2,3],[0,1,3],[2,4,5],[0,2,4],[0,2,3],[0,1,5],[0,2,3],[0,1,5],[2,3,4],[2,3,4],[0,1,3],[0,1,4],[1,2,5],[1,2,3],[0,2,4],[0,2,4],[1,2,5],[1,2,5],[0,2,3],[0,3,4],[0,1,2],[1,3,4],[0,3,4],[1,2,5],[0,1,4],[0,1,4],[0,1,4],[2,4,5],[1,3,4],[2,3,5],[0,1,2],[1,2,5],[0,2,5],[0,2,3],[3,4,5],[0,1,2],[0,1,4],[0,4,5],[1,2,4],[0,4,5],[3,4,5],[1,3,5],[1,3,5],[2,4,5],[1,4,5],[3,4,5],[0,2,5],[0,1,2],[1,3,5],[3,4,5],[0,3,4],[0,1,4],[2,3,5],[1,2,4],[0,2,5],[0,2,3],[0,4,5],[0,1,4],[0,1,4],[1,3,4],[0,1,2],[0,2,5],[0,1,3],[2,4,5],[3,4,5],[1,3,5],[0,2,4],[1,2,5],[1,4,5],[1,2,4],[1,3,5],[0,3,5],[0,4,5],[0,1,4],[2,3,5],[0,1,4],[0,1,2],[1,3,5],[0,3,5],[1,4,5],[0,3,5],[2,3,4],[2,3,5],[1,2,4],[1,4,5],[2,3,5],[2,4,5],[1,3,4],[2,3,5],[1,2,3],[2,3,4],[0,1,2],[0,1,5],[1,2,3],[0,1,5],[2,3,4],[0,3,5],[0,3,4],[1,3,5],[2,4,5],[1,3,4],[2,3,4],[0,3,5],[1,3,5],[1,2,3],[3,4,5],[0,2,4],[0,1,2],[2,3,5],[2,4,5],[0,4,5],[0,2,4],[0,3,4],[1,3,4],[1,2,4],[0,2,5],[1,4,5],[3,4,5],[0,3,4],[2,4,5],[0,1,4],[1,3,5],[2,3,4],[0,1,3],[1,2,5],[1,2,4],[0,2,5],[0,2,4],[0,1,3],[1,4,5],[1,2,4],[1,2,4],[1,2,3],[1,2,4],[0,1,2],[0,2,5],[0,2,5],[0,3,5],[1,2,4],[0,1,4],[1,2,5],[0,2,5],[2,3,5],[0,1,3],[0,3,4],[0,1,2],[1,3,5],[0,1,5],[0,1,5],[0,1,5],[1,2,4],[2,3,5],[0,1,3],[0,1,4],[0,3,5],[0,2,5],[2,4,5],[3,4,5],[3,4,5],[1,3,4],[1,3,5],[2,3,4],[2,3,4]],[[0,4,5],[2,3,5],[0,1,5],[0,3,4],[1,2,5],[1,3,5],[0,1,4],[1,3,5],[0,3,5],[1,2,3],[1,2,3],[1,3,4],[0,1,4],[0,2,4],[2,3,5],[0,1,2],[0,1,3],[0,1,5],[1,2,5],[0,3,4],[1,3,4],[2,3,5],[0,1,3],[1,4,5],[2,4,5],[0,2,4],[0,2,5],[0,3,4],[1,2,3],[1,2,4],[0,1,5],[0,1,5],[3,4,5],[0,4,5],[0,2,3],[1,4,5],[1,2,4],[1,3,4],[0,2,4],[0,2,4],[0,1,4],[1,2,4],[0,1,5],[0,1,5],[0,1,4],[1,3,5],[0,4,5],[3,4,5],[2,4,5],[0,2,5],[0,3,5],[0,1,2],[0,4,5],[1,2,3],[2,3,4],[0,1,2],[0,3,4],[1,3,5],[2,3,4],[0,2,3],[0,3,4],[0,1,3],[1,2,3],[2,3,5],[2,4,5],[1,3,5],[0,4,5],[1,3,4],[0,1,3],[1,3,5],[0,1,5],[0,1,2],[1,2,5],[0,4,5],[0,3,5],[0,2,3],[0,3,5],[0,1,4],[2,4,5],[2,3,5],[0,1,3],[2,4,5],[0,2,5],[0,1,5],[1,2,4],[0,1,3],[1,4,5],[2,3,5],[2,3,5],[0,2,4],[0,2,3],[2,3,4],[0,4,5],[1,4,5],[0,2,3],[0,2,4],[0,1,2],[0,3,4],[0,3,4],[1,4,5],[0,3,5],[3,4,5],[2,3,5],[0,4,5],[0,1,2],[0,3,5],[3,4,5],[1,3,5],[2,4,5],[1,3,5],[1,4,5],[0,1,5],[2,4,5],[2,3,5],[0,1,4],[0,2,3],[3,4,5],[2,3,4],[0,3,5],[0,1,2],[2,3,5],[0,1,4],[1,2,4],[0,2,3],[0,1,3],[0,2,3],[0,1,4],[1,4,5],[0,1,5],[2,3,5],[2,3,5],[3,4,5],[0,2,4],[0,2,4],[1,2,4],[1,2,3],[1,2,3],[0,2,4],[0,2,4],[1,4,5],[0,3,5],[1,2,4],[0,2,4],[1,2,4],[0,2,4],[0,1,3],[1,2,3],[0,1,5],[1,2,4],[1,2,4],[2,4,5],[0,1,3],[0,1,5],[2,4,5],[1,2,3],[0,3,5],[0,4,5],[1,3,4],[0,4,5],[0,1,2],[2,3,4],[1,2,4],[0,1,4],[2,3,5],[1,2,5],[1,2,4],[0,1,5],[0,2,4],[0,1,4],[0,3,5],[1,4,5],[0,3,4],[0,2,3],[0,1,2],[0,1,3],[0,2,5],[2,4,5],[0,2,3],[0,3,5],[0,1,3],[2,3,5],[0,3,4],[0,3,5],[1,2,3],[0,2,4],[2,3,4],[0,3,5],[2,3,4],[1,3,5],[2,3,5],[1,2,4],[1,3,5],[1,3,4],[1,3,4],[0,1,3],[0,1,3],[0,2,3],[0,3,4],[0,2,4],[0,1,3],[0,1,3],[1,3,4],[0,1,3],[0,3,5],[0,3,5],[0,1,3],[1,3,5],[2,4,5],[2,3,5],[2,4,5],[1,3,5],[1,2,5],[0,3,5],[2,3,5],[0,2,4],[0,1,4],[1,3,5],[2,3,4],[3,4,5],[0,1,4],[0,1,5],[1,3,4],[1,3,5],[1,3,4],[0,1,4],[0,2,4],[1,2,5],[2,3,5],[1,4,5],[2,4,5],[0,1,5],[0,3,5],[0,1,4],[0,3,5],[1,2,3],[1,3,4],[1,2,3],[1,3,5],[1,4,5],[0,3,4],[3,4,5],[1,3,4],[1,2,3],[1,2,4],[1,4,5],[2,4,5],[1,2,4],[0,3,4],[0,2,4],[2,3,4],[0,2,4],[0,2,4],[0,1,5],[0,2,3],[0,1,3],[1,2,5],[0,1,5],[1,3,5],[1,2,4],[1,2,5],[2,3,5],[0,1,5],[0,3,4],[1,2,4],[2,3,5],[2,3,5],[3,4,5],[0,4,5],[0,4,5],[0,2,5],[2,3,5],[1,2,4],[1,3,5],[0,1,2],[1,3,5],[0,2,5],[2,3,5],[0,4,5],[1,2,5],[1,2,3],[0,1,3],[2,4,5],[0,3,4],[0,1,4],[0,1,5],[0,2,5],[1,3,4],[2,4,5],[2,4,5],[0,2,4],[1,3,5],[2,3,5],[3,4,5],[3,4,5],[1,3,5],[1,4,5],[0,3,4],[0,2,4],[0,2,3],[1,2,5],[0,3,4],[3,4,5],[1,2,3],[1,2,3],[0,2,5],[2,3,5],[2,3,5],[3,4,5],[2,4,5],[0,1,2],[1,4,5],[0,1,4],[0,1,3],[1,3,5],[0,4,5],[0,2,5],[0,1,3],[1,2,3],[1,2,3],[1,3,4],[1,3,5],[1,2,5],[1,3,5],[3,4,5],[3,4,5],[0,2,5],[1,2,3],[0,3,4],[1,2,3],[3,4,5],[3,4,5],[1,2,3],[1,3,4],[2,4,5],[1,2,4],[2,4,5],[0,1,5],[0,2,4],[1,3,4],[1,2,5],[1,2,4],[0,1,3],[1,2,5],[0,2,3],[2,4,5],[2,3,4],[0,2,4],[2,4,5],[1,2,3],[0,1,5],[0,3,4],[2,3,5],[0,3,5],[2,4,5],[0,1,3],[2,4,5],[0,3,4],[0,4,5],[3,4,5],[0,4,5],[1,2,5],[0,2,4],[1,3,4],[1,3,4],[2,3,5],[0,3,5],[0,2,3],[0,1,2],[2,3,5],[2,3,4],[2,3,4],[2,4,5],[1,2,4],[1,3,4],[0,1,4],[1,4,5],[0,2,3],[1,3,5],[0,1,4],[1,3,5],[1,2,3],[1,2,5],[2,3,5],[0,4,5],[3,4,5],[0,2,4],[0,3,4],[0,1,4],[1,3,5],[2,3,4],[1,2,3],[1,2,4],[0,2,5],[2,3,4],[3,4,5],[1,2,5],[0,1,4],[0,2,3],[2,4,5],[0,3,4],[0,1,5],[1,3,5],[1,3,5],[2,3,5],[2,3,5],[0,2,5],[0,3,5],[0,2,3],[0,1,3],[0,1,2],[3,4,5],[2,4,5],[0,3,4],[0,1,2],[3,4,5],[1,4,5],[0,1,5],[1,2,5],[0,1,2],[0,1,4],[0,1,3],[0,3,5],[0,2,3],[0,2,3],[0,3,5],[0,2,3],[2,3,5],[0,2,4],[2,3,5],[2,3,5],[3,4,5],[1,3,5],[0,4,5],[0,1,4],[0,2,4],[0,2,5],[2,3,4],[3,4,5],[0,2,5],[1,3,5],[0,2,5],[0,1,3],[0,1,2],[2,4,5],[0,2,5],[0,1,2],[1,3,4],[1,2,4],[2,3,4],[0,1,5],[2,3,4],[0,1,5],[3,4,5],[1,2,4],[2,4,5],[0,1,5],[0,1,4],[2,3,4],[0,1,2],[0,1,3],[3,4,5],[0,1,3],[0,1,2],[1,4,5],[2,3,4],[0,1,3],[0,3,5],[0,2,4],[1,4,5],[1,2,3],[2,4,5],[0,2,4],[0,2,5],[0,2,5],[0,1,5],[0,2,3],[1,2,5],[0,4,5],[1,4,5],[2,4,5],[0,2,3],[2,4,5],[0,2,4],[3,4,5],[2,4,5],[0,2,3],[2,3,5],[1,2,3],[1,3,5],[1,2,3],[2,3,5],[2,3,5],[0,1,2],[1,3,4],[0,4,5],[0,2,3],[1,4,5],[0,1,5],[0,1,3],[2,3,4],[0,3,4],[0,3,5],[0,2,5],[1,2,3],[2,3,5],[0,2,4],[1,2,3],[0,2,4],[0,1,3],[2,3,5],[0,3,4],[0,1,3]],[[0,2,3],[1,4,5],[0,3,4],[0,1,2],[0,2,4],[2,3,4],[1,3,4],[1,2,5],[1,4,5],[0,1,3],[0,1,4],[1,2,4],[1,2,3],[0,1,3],[1,3,4],[3,4,5],[0,1,3],[1,3,5],[2,4,5],[1,3,5],[0,4,5],[1,3,4],[1,2,4],[1,2,3],[0,2,5],[3,4,5],[0,1,3],[2,4,5],[0,2,4],[1,2,3],[1,2,4],[1,2,3],[0,3,5],[0,2,5],[0,4,5],[1,3,5],[0,3,4],[2,3,5],[0,2,4],[1,2,5],[0,3,4],[0,3,5],[0,2,4],[2,3,5],[3,4,5],[0,1,4],[0,2,3],[0,1,4],[2,4,5],[2,3,5],[1,3,4],[0,3,5],[2,3,4],[0,1,4],[1,4,5],[0,1,5],[0,3,4],[2,3,4],[0,2,4],[0,1,2],[2,3,4],[1,2,4],[0,4,5],[1,4,5],[0,2,5],[1,3,4],[0,4,5],[1,2,3],[1,2,3],[0,1,5],[3,4,5],[2,4,5],[1,2,4],[0,1,4],[1,3,4],[0,2,4],[0,3,5],[3,4,5],[0,2,5],[0,3,4],[0,4,5],[2,3,4],[0,1,4],[0,2,3],[2,4,5],[0,1,4],[0,3,4],[0,1,2],[0,1,2],[0,1,3],[0,3,5],[0,1,3],[0,4,5],[0,1,5],[1,3,5],[3,4,5],[1,2,3],[0,2,3],[2,3,5],[0,1,4],[0,1,3],[1,2,5],[1,2,3],[0,1,5],[0,4,5],[1,2,4],[0,4,5],[1,4,5],[0,4,5],[1,2,5],[2,3,4],[0,1,2],[0,1,5],[3,4,5],[2,3,4],[0,1,5],[2,3,5],[0,2,5],[0,2,3],[1,2,5],[3,4,5],[2,3,4],[2,3,5],[0,1,3],[0,2,5],[3,4,5],[3,4,5],[0,1,3],[0,3,5],[1,2,3],[1,4,5],[0,1,5],[0,2,5],[0,1,5],[0,3,5],[0,3,5],[0,1,4],[0,3,5],[0,1,5],[0,1,4],[0,1,4],[2,4,5],[1,4,5],[2,3,4],[1,2,4],[1,2,3],[1,2,5],[0,1,4],[2,4,5],[2,4,5],[0,1,4],[1,3,5],[1,2,3],[0,1,2],[1,2,4],[1,3,4],[0,2,3],[0,1,4],[1,2,4],[1,2,4],[1,2,5],[3,4,5],[0,1,5],[0,3,5],[0,1,2],[1,3,4],[0,2,5],[0,3,4],[0,3,4],[0,3,4],[2,4,5],[1,2,4],[0,1,4],[2,3,4],[2,3,4],[1,3,4],[0,2,3],[1,4,5],[1,4,5],[2,4,5],[1,2,5],[1,3,4],[1,4,5],[0,2,4],[1,2,3],[1,2,5],[1,2,5],[1,2,5],[1,3,5],[0,1,5],[1,3,5],[0,4,5],[1,2,3],[0,1,3],[1,2,3],[1,4,5],[0,2,5],[0,1,5],[1,4,5],[0,2,4],[0,3,5],[0,3,5],[1,2,3],[0,2,3],[1,2,3],[0,1,2],[0,3,5],[0,1,2],[1,2,3],[0,2,5],[3,4,5],[2,3,4],[0,1,5],[0,3,4],[0,4,5],[0,1,3],[0,3,5],[1,3,5],[1,4,5],[1,4,5],[1,3,4],[0,4,5],[0,1,5],[0,1,2],[1,2,3],[0,1,2],[1,4,5],[2,3,5],[0,2,5],[2,3,5],[0,1,3],[0,1,4],[0,2,5],[0,2,3],[1,3,4],[3,4,5],[1,3,4],[2,3,5],[1,3,5],[1,2,5],[3,4,5],[0,1,5],[1,3,5],[0,1,3],[0,2,5],[0,3,4],[0,1,3],[1,3,4],[3,4,5],[1,3,5],[1,4,5],[0,4,5],[0,1,3],[0,1,3],[0,3,5],[2,3,5],[0,1,5],[2,3,5],[0,1,4],[2,3,5],[0,3,5],[3,4,5],[2,4,5],[1,2,4],[0,1,4],[1,4,5],[0,1,2],[0,2,4],[0,2,3],[0,3,4],[0,1,2],[1,2,4],[0,1,3],[0,2,5],[0,4,5],[1,4,5],[1,3,5],[0,2,4],[1,2,5],[0,2,3],[0,4,5],[0,1,2],[1,2,4],[1,2,4],[0,2,3],[1,2,4],[1,2,5],[0,1,5],[0,2,4],[1,2,5],[0,2,5],[0,2,4],[1,4,5],[0,2,4],[0,2,5],[0,1,5],[1,3,4],[3,4,5],[1,2,4],[0,1,5],[0,1,2],[0,2,3],[0,4,5],[0,1,2],[0,1,3],[0,4,5],[1,2,5],[0,1,2],[3,4,5],[0,1,2],[0,2,5],[0,1,5],[0,2,3],[2,3,4],[0,3,5],[0,2,4],[0,1,4],[0,1,5],[0,1,4],[3,4,5],[0,1,5],[0,1,4],[0,3,4],[0,3,4],[1,4,5],[1,3,5],[1,2,4],[0,1,4],[2,3,5],[1,3,4],[0,2,5],[2,3,5],[1,3,4],[3,4,5],[2,4,5],[2,3,4],[0,2,4],[2,3,4],[0,4,5],[0,2,4],[0,1,4],[0,3,5],[0,3,5],[2,3,4],[0,2,4],[0,4,5],[0,1,5],[0,1,5],[1,2,3],[1,2,4],[1,2,5],[1,2,5],[0,1,2],[0,3,4],[1,4,5],[1,2,3],[1,3,5],[0,2,5],[0,3,5],[0,1,4],[0,2,3],[1,2,4],[1,2,5],[0,2,3],[3,4,5],[1,2,4],[1,3,4],[1,3,5],[1,3,4],[1,2,4],[0,1,2],[0,1,5],[1,2,3],[1,2,3],[0,2,3],[0,3,4],[0,1,3],[1,3,4],[1,2,3],[1,3,4],[0,2,3],[1,4,5],[0,1,4],[0,1,2],[1,3,4],[1,3,4],[2,4,5],[1,3,4],[0,1,2],[1,4,5],[3,4,5],[3,4,5],[0,1,4],[1,3,5],[3,4,5],[0,1,3],[0,2,5],[1,2,4],[1,2,5],[0,1,5],[1,3,5],[3,4,5],[0,4,5],[0,3,5],[0,2,4],[2,3,4],[0,1,4],[0,4,5],[0,1,4],[0,2,4],[0,1,5],[2,3,5],[1,4,5],[1,2,4],[0,2,5],[0,1,3],[1,2,5],[1,2,5],[0,2,3],[1,4,5],[1,2,4],[1,2,4],[0,1,5],[0,3,5],[2,3,4],[2,3,4],[0,1,3],[3,4,5],[1,3,4],[0,3,5],[2,3,4],[0,2,5],[0,3,4],[0,3,5],[0,3,5],[1,3,5],[3,4,5],[2,3,4],[1,2,3],[0,1,5],[0,3,5],[0,3,4],[0,2,4],[1,2,4],[2,4,5],[1,3,5],[0,1,3],[2,3,5],[0,3,4],[0,1,3],[1,2,3],[3,4,5],[3,4,5],[0,1,4],[0,1,3],[2,3,4],[0,1,5],[0,2,4],[0,2,3],[0,4,5],[2,3,4],[0,1,3],[0,4,5],[3,4,5],[1,2,5],[1,3,4],[2,4,5],[0,1,4],[1,3,5],[0,1,2],[1,2,3],[2,3,5],[0,1,2],[0,3,5],[2,3,5],[2,3,4],[0,1,2],[0,2,4],[2,4,5],[1,3,4],[0,1,5],[0,2,3],[0,2,4],[2,4,5],[3,4,5],[0,2,5],[0,3,4],[0,1,5],[1,2,4],[2,3,4],[2,3,4],[0,1,3],[0,3,5],[2,3,4],[2,3,4],[0,1,3],[0,2,4],[0,2,3],[0,4,5],[0,1,3],[0,4,5],[2,3,4],[0,2,3],[1,3,5],[0,1,5],[2,3,5],[1,3,4],[1,4,5],[0,3,5],[0,3,5],[0,1,5],[1,3,5]],[[0,3,4],[0,1,5],[0,1,3],[1,2,4],[0,1,2],[2,4,5],[0,2,4],[1,2,4],[1,2,5],[1,3,4],[1,2,4],[0,3,4],[1,3,5],[0,1,4],[1,2,4],[0,3,4],[2,4,5],[0,2,4],[1,2,4],[1,2,3],[0,2,3],[1,3,5],[0,1,3],[0,2,4],[1,3,5],[0,1,2],[1,3,5],[0,2,5],[1,2,5],[1,2,3],[0,3,5],[0,3,4],[0,1,2],[3,4,5],[1,3,4],[1,3,4],[1,3,4],[1,2,4],[0,1,4],[0,1,2],[0,1,5],[1,3,4],[3,4,5],[0,3,4],[0,1,5],[1,3,4],[1,3,5],[1,4,5],[1,2,3],[0,2,4],[0,1,4],[1,2,3],[1,4,5],[1,4,5],[0,2,4],[1,3,4],[0,2,5],[0,2,3],[0,3,5],[1,4,5],[0,1,2],[0,1,5],[2,4,5],[1,2,5],[2,3,4],[0,1,2],[2,3,4],[1,3,5],[0,1,3],[1,2,3],[1,3,5],[0,3,5],[1,2,4],[1,2,4],[1,2,5],[0,2,3],[1,3,5],[0,2,5],[0,1,4],[1,3,5],[0,1,4],[0,3,4],[0,2,4],[0,1,5],[0,3,4],[1,2,5],[0,3,4],[0,2,5],[0,1,3],[3,4,5],[1,4,5],[1,4,5],[0,3,4],[0,2,5],[1,2,5],[0,2,5],[0,1,2],[0,1,4],[2,3,5],[0,1,5],[1,3,5],[0,1,4],[0,2,3],[2,4,5],[0,2,3],[1,3,4],[0,1,5],[0,4,5],[0,4,5],[0,2,4],[0,1,3],[0,2,5],[0,1,2],[1,3,5],[0,1,3],[0,2,4],[0,1,5],[2,3,4],[0,3,4],[1,2,3],[0,4,5],[0,1,4],[0,1,3],[1,2,5],[0,4,5],[0,1,4],[0,2,4],[0,1,2],[0,1,5],[0,2,4],[2,3,5],[2,3,5],[0,4,5],[0,1,2],[2,3,4],[0,2,5],[0,2,4],[1,4,5],[2,4,5],[1,2,5],[1,2,3],[0,3,5],[0,2,4],[2,3,5],[3,4,5],[1,2,4],[0,1,4],[1,3,5],[2,3,5],[0,3,5],[0,1,4],[1,3,4],[1,2,5],[0,1,2],[0,4,5],[0,2,3],[0,3,4],[0,1,4],[0,1,4],[0,1,2],[0,4,5],[0,2,3],[1,3,5],[1,4,5],[0,3,5],[0,1,5],[1,3,5],[2,3,4],[1,2,3],[2,3,4],[1,3,4],[0,3,5],[1,2,4],[0,1,4],[2,3,4],[0,4,5],[0,1,2],[0,1,4],[2,3,4],[1,4,5],[1,3,5],[0,2,3],[0,1,4],[3,4,5],[0,4,5],[1,2,5],[0,4,5],[0,1,3],[1,3,5],[1,2,3],[1,2,5],[1,3,5],[3,4,5],[1,2,5],[3,4,5],[2,3,5],[1,2,3],[1,2,4],[0,3,4],[0,1,4],[0,1,5],[0,1,3],[1,3,4],[0,1,4],[0,2,3],[0,2,3],[0,1,2],[1,3,5],[2,3,4],[0,1,5],[0,1,2],[0,3,4],[1,3,4],[1,3,5],[1,2,4],[0,1,3],[1,3,5],[0,3,4],[2,3,4],[3,4,5],[2,3,4],[0,4,5],[1,2,3],[0,1,3],[0,1,3],[2,4,5],[0,2,4],[1,4,5],[2,3,5],[1,2,5],[0,1,2],[3,4,5],[1,3,5],[0,1,5],[1,3,5],[1,2,3],[0,1,3],[0,1,3],[0,2,4],[1,2,5],[0,1,3],[0,1,2],[1,2,5],[2,3,5],[0,1,4],[0,1,5],[1,2,5],[0,1,2],[0,2,4],[1,3,5],[0,1,2],[0,2,4],[1,3,5],[1,2,4],[0,1,5],[2,4,5],[0,2,5],[0,1,3],[0,1,2],[0,4,5],[0,1,4],[3,4,5],[0,4,5],[1,2,4],[0,3,5],[1,2,3],[1,2,5],[1,2,5],[2,4,5],[3,4,5],[1,2,4],[1,2,3],[0,2,5],[1,2,4],[0,3,4],[1,2,5],[1,4,5],[1,3,5],[0,1,5],[0,4,5],[1,3,5],[0,3,4],[1,3,5],[0,2,3],[1,3,4],[0,3,4],[2,3,4],[3,4,5],[0,3,5],[1,2,4],[3,4,5],[1,4,5],[0,2,5],[2,3,4],[0,1,2],[0,1,4],[0,2,4],[0,3,4],[0,4,5],[1,3,5],[2,3,5],[1,4,5],[2,4,5],[2,3,4],[0,1,5],[2,4,5],[0,4,5],[0,2,4],[0,1,3],[0,1,4],[2,3,4],[1,2,4],[1,2,5],[2,3,4],[2,3,4],[1,4,5],[2,4,5],[2,4,5],[1,3,5],[2,4,5],[0,1,4],[0,3,4],[1,2,3],[0,4,5],[0,2,5],[0,2,5],[2,4,5],[1,4,5],[0,1,5],[0,3,5],[0,1,2],[1,3,5],[0,4,5],[1,4,5],[2,4,5],[0,2,4],[0,2,4],[0,1,3],[1,4,5],[0,1,5],[1,2,5],[1,2,4],[0,1,3],[0,2,5],[1,2,5],[1,2,4],[1,2,4],[2,3,5],[1,2,5],[1,2,5],[1,2,3],[0,4,5],[1,4,5],[2,3,4],[0,3,4],[1,2,3],[0,1,2],[1,3,5],[0,1,2],[1,2,5],[0,2,4],[0,1,2],[0,3,5],[0,1,4],[0,2,4],[0,1,5],[0,2,4],[3,4,5],[1,2,5],[1,3,4],[0,1,4],[0,3,4],[2,3,5],[0,2,5],[2,4,5],[0,2,5],[2,4,5],[1,2,5],[1,2,5],[0,2,5],[2,3,5],[0,1,2],[3,4,5],[0,1,5],[0,1,2],[0,1,3],[0,2,3],[1,4,5],[1,2,3],[1,4,5],[1,3,4],[1,2,5],[0,1,2],[2,4,5],[1,2,3],[1,4,5],[0,1,4],[0,1,3],[0,1,5],[1,3,4],[1,2,3],[0,1,3],[1,4,5],[1,2,4],[2,3,4],[0,2,3],[0,2,4],[0,2,4],[0,1,5],[1,4,5],[0,1,2],[3,4,5],[0,1,3],[0,3,4],[1,2,4],[0,4,5],[2,4,5],[0,1,2],[1,3,4],[0,3,5],[0,1,5],[1,3,4],[1,2,4],[1,4,5],[1,2,3],[0,3,5],[0,1,3],[2,3,4],[3,4,5],[0,1,3],[0,1,5],[2,4,5],[3,4,5],[2,3,5],[1,2,4],[2,4,5],[2,3,5],[3,4,5],[1,3,4],[0,1,3],[0,1,3],[0,3,4],[1,4,5],[0,2,5],[0,1,3],[0,3,5],[3,4,5],[1,4,5],[0,3,4],[0,2,4],[2,3,5],[0,2,5],[0,1,4],[0,1,3],[1,3,4],[3,4,5],[0,3,4],[0,1,3],[0,1,3],[0,1,3],[0,2,4],[2,4,5],[0,1,3],[2,4,5],[2,3,4],[1,2,5],[0,1,3],[1,3,4],[0,2,3],[2,4,5],[2,4,5],[1,2,5],[1,3,5],[0,1,2],[0,3,5],[0,2,5],[0,2,3],[0,1,5],[0,2,5],[2,4,5],[0,1,5],[1,2,5],[0,1,4],[0,1,3],[1,3,4],[0,2,5],[0,1,2],[1,2,3],[0,3,4],[1,4,5],[0,4,5],[0,1,3],[1,2,5],[1,3,5],[1,4,5],[1,2,4],[0,1,5],[0,2,3],[1,2,5],[0,1,3],[1,2,3],[1,2,3],[1,2,3],[0,2,3],[2,4,5],[1,3,5],[1,3,4],[0,2,4],[0,1,3],[1,2,4],[0,3,5],[1,2,4]],[[0,4,5],[0,2,4],[1,2,5],[1,3,5],[3,4,5],[1,3,4],[0,2,3],[2,3,4],[2,4,5],[2,3,4],[0,4,5],[2,4,5],[1,2,3],[0,3,4],[0,2,5],[1,2,4],[0,1,3],[0,3,5],[2,3,5],[1,4,5],[0,2,4],[0,2,3],[0,2,4],[0,1,3],[2,3,4],[0,3,5],[2,4,5],[0,3,5],[0,2,4],[2,3,4],[0,3,5],[0,1,5],[3,4,5],[1,2,5],[1,2,5],[0,1,3],[0,1,2],[0,1,4],[0,2,5],[0,3,5],[0,1,5],[1,3,5],[1,2,4],[2,3,4],[0,4,5],[2,3,4],[0,1,2],[1,3,5],[1,2,4],[0,2,3],[0,2,5],[1,2,3],[1,2,3],[0,3,4],[2,3,5],[0,2,3],[0,1,3],[1,3,4],[0,3,4],[0,2,5],[1,3,5],[0,1,2],[1,4,5],[1,2,5],[2,3,4],[0,1,4],[2,3,4],[1,2,5],[0,1,5],[0,4,5],[1,2,4],[0,1,3],[2,3,5],[0,4,5],[0,4,5],[0,1,2],[1,2,3],[2,3,4],[0,1,3],[0,2,3],[0,4,5],[2,3,5],[2,3,5],[2,3,4],[2,4,5],[0,2,4],[1,4,5],[0,1,4],[1,2,5],[1,2,5],[1,3,5],[1,2,4],[0,1,5],[0,1,5],[1,3,5],[0,2,4],[1,3,4],[3,4,5],[0,1,5],[1,3,4],[1,2,4],[0,1,5],[0,2,3],[2,3,4],[2,4,5],[1,4,5],[0,3,4],[1,2,4],[1,2,4],[2,3,4],[0,2,5],[1,2,3],[1,2,4],[0,4,5],[0,3,4],[0,2,4],[1,2,5],[1,3,5],[1,2,5],[1,2,4],[0,2,4],[0,4,5],[1,3,4],[0,2,5],[0,3,5],[0,1,5],[0,2,3],[2,4,5],[0,1,2],[0,1,2],[0,1,2],[1,3,4],[0,2,5],[2,3,5],[2,3,4],[1,3,4],[0,3,5],[0,1,5],[0,2,4],[0,2,5],[2,3,4],[0,1,2],[0,2,5],[2,3,5],[0,1,2],[0,4,5],[0,3,4],[0,2,4],[0,3,4],[0,1,4],[2,3,5],[1,4,5],[0,4,5],[0,2,5],[0,1,2],[2,3,5],[1,2,4],[2,4,5],[0,3,5],[0,2,5],[1,2,3],[0,2,4],[0,1,3],[2,4,5],[2,3,5],[0,1,5],[0,1,4],[0,2,5],[1,3,5],[1,3,5],[0,2,4],[2,3,5],[0,4,5],[2,3,5],[1,3,5],[0,2,3],[1,3,5],[1,2,4],[1,2,4],[0,1,4],[0,1,4],[1,2,3],[0,1,5],[0,4,5],[0,2,4],[2,3,5],[1,3,5],[0,2,4],[0,1,3],[1,3,4],[1,2,4],[0,1,5],[1,4,5],[3,4,5],[0,1,4],[0,3,5],[0,3,5],[0,1,5],[0,1,4],[0,3,4],[3,4,5],[1,4,5],[0,4,5],[1,2,5],[0,3,5],[0,1,2],[1,2,3],[1,2,5],[0,2,4],[0,3,5],[2,3,4],[0,2,4],[2,3,4],[3,4,5],[0,3,4],[0,3,4],[0,1,3],[0,3,4],[1,2,3],[0,4,5],[1,2,3],[1,3,5],[1,4,5],[1,3,4],[0,2,4],[1,3,4],[0,1,5],[3,4,5],[0,3,5],[0,2,3],[2,3,4],[1,2,5],[0,3,5],[3,4,5],[0,2,3],[1,3,5],[0,4,5],[0,2,4],[1,2,4],[0,2,4],[1,2,4],[0,3,4],[0,1,3],[0,1,2],[0,1,5],[0,1,3],[0,2,5],[1,2,5],[0,4,5],[1,2,4],[0,2,5],[0,1,2],[0,1,3],[0,1,3],[0,1,5],[1,3,5],[1,2,3],[0,1,3],[3,4,5],[1,2,5],[0,1,3],[2,4,5],[2,4,5],[2,4,5],[1,2,3],[0,3,5],[3,4,5],[0,2,4],[0,3,5],[2,4,5],[1,3,4],[1,2,5],[2,3,5],[0,2,5],[1,2,3],[0,2,4],[1,2,3],[0,1,5],[1,2,4],[0,1,2],[0,1,4],[1,3,4],[1,2,5],[1,2,5],[0,1,4],[0,4,5],[0,2,5],[2,3,4],[2,3,4],[3,4,5],[1,2,3],[1,3,4],[1,3,4],[1,2,3],[0,1,3],[1,2,4],[0,1,2],[2,3,5],[1,2,3],[0,1,3],[2,3,5],[1,3,5],[1,4,5],[2,4,5],[1,2,5],[1,3,5],[0,2,3],[0,1,3],[3,4,5],[0,1,2],[1,2,3],[3,4,5],[1,3,5],[0,3,4],[0,4,5],[0,1,2],[0,2,4],[1,2,4],[0,3,5],[0,1,5],[0,1,2],[0,1,3],[0,3,4],[2,3,4],[0,4,5],[1,3,5],[1,3,4],[1,2,5],[1,3,4],[1,2,4],[1,2,5],[0,2,5],[0,3,5],[1,3,4],[0,2,3],[0,1,3],[0,1,4],[0,4,5],[2,3,5],[0,3,5],[1,3,4],[1,2,3],[2,3,5],[0,4,5],[0,1,5],[2,3,5],[0,1,5],[1,2,4],[1,4,5],[0,2,3],[1,3,5],[0,1,4],[0,3,4],[3,4,5],[0,1,3],[1,2,5],[0,3,4],[0,2,3],[1,3,4],[0,2,5],[2,4,5],[0,1,4],[0,1,3],[0,1,3],[0,1,2],[0,2,3],[0,3,5],[2,3,5],[2,4,5],[0,4,5],[2,3,5],[0,1,4],[1,2,3],[0,1,2],[0,2,3],[2,4,5],[0,1,5],[0,1,4],[0,2,4],[1,2,4],[0,2,4],[0,1,3],[0,2,4],[0,1,4],[0,2,4],[2,3,4],[0,1,3],[1,2,5],[2,3,4],[0,3,5],[0,2,4],[0,1,3],[0,1,3],[3,4,5],[0,1,3],[3,4,5],[0,1,3],[1,2,5],[2,4,5],[0,1,5],[3,4,5],[2,3,5],[0,1,3],[0,1,2],[0,1,3],[1,3,4],[1,4,5],[2,4,5],[1,2,5],[1,2,5],[1,2,3],[0,1,4],[0,1,4],[0,1,5],[1,3,4],[3,4,5],[3,4,5],[1,3,5],[0,1,4],[1,3,4],[1,3,4],[1,2,5],[0,1,3],[0,1,5],[0,1,3],[0,3,5],[0,1,4],[0,2,5],[0,4,5],[1,3,4],[1,2,5],[3,4,5],[0,3,4],[3,4,5],[1,3,4],[2,3,5],[1,2,4],[2,3,5],[0,3,4],[2,3,5],[0,1,3],[1,4,5],[0,2,3],[1,2,4],[1,2,4],[0,1,3],[1,2,3],[1,4,5],[1,2,4],[0,1,4],[1,4,5],[0,4,5],[3,4,5],[1,4,5],[0,1,3],[1,3,5],[0,1,5],[0,1,5],[0,2,3],[0,1,5],[1,3,4],[0,3,5],[0,1,2],[1,2,5],[3,4,5],[2,3,5],[0,1,3],[1,3,5],[0,3,4],[0,1,2],[3,4,5],[0,1,2],[0,2,3],[0,1,2],[2,3,5],[1,2,3],[0,1,4],[2,4,5],[0,1,5],[1,3,4],[3,4,5],[2,3,5],[0,1,3],[1,2,4],[0,3,4],[0,1,3],[0,2,4],[0,2,5],[1,2,5],[0,2,3],[0,1,3],[1,2,4],[1,2,5],[0,1,3],[0,2,5],[0,3,5],[2,3,5],[2,3,5],[3,4,5],[1,4,5],[1,2,3],[2,4,5],[0,3,4],[1,2,5],[0,3,5],[1,2,5],[1,2,3],[0,1,2],[1,3,4],[0,3,4],[2,3,5],[3,4,5]],[[0,3,5],[0,3,5],[1,2,3],[2,3,4],[0,2,3],[1,2,5],[1,2,3],[0,1,5],[1,2,5],[0,3,5],[0,4,5],[0,1,4],[0,1,4],[0,2,5],[2,4,5],[0,1,3],[0,1,4],[0,2,4],[1,2,4],[0,1,4],[0,2,3],[0,1,5],[0,4,5],[2,3,4],[1,3,5],[0,1,4],[0,2,4],[2,3,5],[0,1,4],[2,3,4],[2,4,5],[3,4,5],[3,4,5],[2,3,5],[0,3,4],[0,1,4],[0,4,5],[0,3,5],[0,1,2],[0,3,5],[2,3,4],[1,3,5],[0,2,3],[1,3,4],[0,3,5],[0,1,2],[1,2,5],[0,2,3],[0,1,3],[0,1,5],[2,3,5],[3,4,5],[2,3,4],[3,4,5],[3,4,5],[0,4,5],[0,2,4],[2,4,5],[1,2,5],[2,4,5],[1,2,3],[3,4,5],[0,1,5],[0,3,4],[0,2,5],[2,3,4],[0,4,5],[0,3,5],[1,4,5],[1,2,5],[0,2,4],[0,3,5],[1,3,4],[3,4,5],[0,1,3],[0,1,2],[1,2,4],[0,1,3],[1,3,5],[0,2,4],[3,4,5],[1,4,5],[2,3,4],[0,3,5],[0,1,4],[1,2,4],[0,4,5],[0,1,3],[0,4,5],[1,3,5],[0,2,4],[1,4,5],[0,4,5],[1,4,5],[0,2,4],[0,4,5],[1,4,5],[0,3,5],[2,4,5],[0,3,4],[2,3,4],[0,2,5],[3,4,5],[1,3,5],[1,3,4],[0,4,5],[1,3,4],[0,1,2],[0,2,3],[1,3,4],[0,1,3],[0,2,4],[0,1,4],[2,3,5],[1,4,5],[0,1,3],[0,1,3],[2,4,5],[3,4,5],[1,2,4],[1,2,4],[1,2,3],[0,1,3],[2,4,5],[0,1,2],[0,3,5],[0,4,5],[1,2,4],[0,4,5],[0,1,2],[1,3,4],[0,1,3],[0,1,3],[1,2,3],[1,3,4],[0,4,5],[0,3,4],[1,2,3],[0,3,5],[2,4,5],[0,2,3],[1,3,5],[0,3,4],[0,3,5],[0,1,5],[0,3,5],[2,4,5],[0,3,4],[1,3,5],[0,4,5],[1,3,5],[2,3,4],[0,1,4],[0,1,3],[2,3,5],[2,4,5],[2,4,5],[0,2,3],[0,2,5],[0,2,3],[2,3,5],[0,4,5],[1,3,4],[1,2,4],[0,2,5],[1,4,5],[1,4,5],[1,4,5],[3,4,5],[0,3,5],[0,2,4],[0,4,5],[1,4,5],[0,2,4],[0,2,5],[2,3,5],[2,3,5],[0,1,2],[1,3,5],[0,3,5],[1,2,3],[0,1,3],[0,1,4],[0,2,5],[1,2,4],[2,3,5],[2,3,4],[0,1,2],[0,2,5],[0,1,2],[0,1,4],[0,2,5],[0,2,3],[0,3,4],[0,1,5],[0,1,3],[2,4,5],[3,4,5],[3,4,5],[0,1,4],[2,3,5],[0,1,5],[1,3,5],[3,4,5],[1,3,4],[1,4,5],[0,4,5],[0,3,4],[0,2,4],[0,4,5],[2,4,5],[0,2,3],[0,1,3],[1,2,4],[0,4,5],[1,2,4],[0,2,3],[0,1,4],[1,3,4],[0,1,3],[0,2,5],[0,3,5],[0,2,4],[2,4,5],[1,2,5],[0,4,5],[0,1,4],[1,2,4],[3,4,5],[1,2,4],[1,4,5],[3,4,5],[0,2,3],[0,2,4],[0,4,5],[0,1,4],[2,3,5],[1,2,5],[1,2,5],[2,3,4],[0,1,2],[0,1,4],[1,3,4],[0,3,5],[2,3,5],[1,2,5],[1,2,3],[0,2,3],[2,3,5],[0,1,5],[0,4,5],[0,2,4],[2,3,4],[1,3,5],[1,3,5],[0,1,2],[1,3,5],[0,2,4],[1,3,5],[0,2,5],[0,1,3],[0,3,4],[1,2,3],[0,1,2],[0,1,3],[0,1,2],[1,2,5],[1,2,4],[0,3,5],[0,1,5],[0,2,3],[0,1,3],[0,2,3],[0,3,4],[1,2,5],[1,3,5],[1,2,4],[0,1,5],[1,2,5],[1,2,4],[0,2,3],[3,4,5],[0,2,5],[1,2,3],[1,2,4],[1,2,3],[1,3,5],[2,3,5],[1,2,4],[0,1,4],[2,4,5],[2,3,5],[0,2,4],[0,2,4],[1,4,5],[1,2,3],[0,1,5],[0,1,3],[1,2,4],[0,1,4],[1,3,4],[0,3,5],[0,1,5],[2,3,5],[1,2,5],[0,1,2],[0,2,3],[0,3,5],[0,1,5],[0,3,5],[3,4,5],[1,3,5],[0,1,5],[0,1,4],[0,1,4],[1,2,3],[0,2,4],[0,2,4],[1,3,5],[2,3,5],[2,4,5],[0,1,4],[0,1,3],[1,2,5],[1,3,4],[0,4,5],[0,1,5],[0,3,4],[2,4,5],[1,2,3],[0,2,3],[2,3,4],[2,4,5],[2,3,5],[2,4,5],[0,1,5],[1,3,4],[1,3,4],[0,3,4],[1,2,5],[0,2,5],[0,2,5],[3,4,5],[2,3,4],[0,3,4],[0,2,5],[1,2,4],[1,2,3],[2,4,5],[1,2,5],[0,2,4],[1,3,4],[0,2,5],[1,2,4],[3,4,5],[0,2,4],[1,4,5],[0,1,5],[2,3,4],[3,4,5],[0,1,2],[0,3,4],[2,3,4],[0,4,5],[0,1,5],[0,1,4],[0,1,4],[2,3,4],[2,4,5],[1,3,5],[1,3,4],[0,1,2],[3,4,5],[1,2,4],[0,2,5],[2,4,5],[1,3,5],[0,1,3],[0,2,5],[0,1,5],[0,2,4],[0,2,3],[3,4,5],[2,4,5],[0,1,3],[2,3,4],[1,2,3],[1,2,4],[0,3,5],[1,4,5],[0,4,5],[1,2,3],[1,3,4],[2,3,4],[0,1,5],[1,2,5],[0,1,5],[1,2,4],[0,2,5],[2,3,4],[0,2,5],[1,2,3],[1,3,4],[1,2,5],[1,2,4],[0,2,4],[1,3,5],[0,2,5],[0,2,4],[1,2,5],[1,3,5],[1,3,5],[3,4,5],[0,2,4],[2,3,5],[1,4,5],[0,4,5],[1,3,5],[1,2,3],[1,3,4],[1,2,4],[2,3,5],[0,1,3],[0,1,3],[0,2,3],[0,1,2],[1,3,5],[0,1,3],[0,2,5],[1,3,5],[0,1,2],[2,4,5],[2,3,5],[1,3,5],[0,3,5],[0,2,4],[1,2,4],[1,2,3],[1,3,5],[2,3,5],[0,2,4],[0,1,3],[0,1,4],[0,2,4],[0,2,5],[1,4,5],[0,4,5],[2,4,5],[1,4,5],[0,4,5],[2,4,5],[0,2,5],[0,1,2],[2,3,5],[2,3,4],[0,1,4],[1,2,4],[0,1,3],[0,3,4],[2,4,5],[0,2,5],[0,4,5],[0,1,3],[0,3,5],[2,3,5],[1,2,3],[1,2,5],[0,3,5],[0,2,3],[0,1,2],[1,2,3],[0,1,2],[1,3,4],[2,4,5],[1,4,5],[1,2,4],[0,1,3],[0,3,5],[1,4,5],[1,3,4],[0,1,5],[0,3,4],[3,4,5],[1,2,5],[0,2,4],[0,3,5],[0,2,3],[3,4,5],[2,3,4],[0,1,3],[0,2,5],[1,3,5],[2,3,5],[1,3,5],[1,2,5],[2,3,5],[1,4,5],[0,4,5],[1,3,5],[1,2,5],[1,2,3],[1,4,5],[1,3,4],[0,3,5],[1,2,4],[0,1,3],[0,1,2],[0,4,5],[2,3,5],[0,1,3],[0,3,5],[0,2,4]]]
def setup_inputs(rng):
    return {"x": rng.standard_normal((N, 128, TOK), dtype=np.float32).astype(ml_dtypes.bfloat16), "gate": (0.5 * rng.integers(1, 4, size=(N, K, TOK)) * (2 * rng.integers(0, 2, size=(N, K, TOK)) - 1)).astype(np.float32).astype(ml_dtypes.bfloat16), "w1": (rng.standard_normal((N, 128, FT * 128), dtype=np.float32) / 8).astype(ml_dtypes.bfloat16), "w2": (rng.standard_normal((N, 128, FT * 128), dtype=np.float32) / 8).astype(ml_dtypes.bfloat16)}
def setup_inputs_big(rng):
    d = setup_inputs(rng)
    for k in ("x", "gate", "w1", "w2"): d[k] = (d[k].astype(np.float32) * 1024.0).astype(d[k].dtype)
    return d
def setup_inputs_small(rng):
    d = setup_inputs(rng)
    for k in ("x", "gate", "w1", "w2"): d[k] = (d[k].astype(np.float32) * (1 / 1024.0)).astype(d[k].dtype)
    return d
def reference(x, gate, w1, w2):
    X, GATE, W1, W2 = x.astype(np.float64), gate.astype(np.float64), w1.astype(np.float64), w2.astype(np.float64)
    y = np.zeros((N, 128, TOK))
    for r in range(N):
        for t in range(TOK):
            for i, e in enumerate(ROUTE[r][t]):
                hid = np.maximum(W1[e].T @ X[r][:, t], 0.0)
                y[r][:, t] += GATE[r][i, t] * sum(W2[e][:, 128 * f:128 * f + 128].T @ hid[128 * f:128 * f + 128] for f in range(FT))
    return {"y": y.astype(ml_dtypes.bfloat16)}

@@ -1,0 +1,326 @@
+from concourse.mybir import dt, AluOpType
+
+NSIM = 256
+TOKS = 512
+HALF = 256
+NR = 6
+
+SCRATCH = {
+    "wall": ("sbuf", [128, NR * 256], "bfloat16"),
+    "rb":   ("sbuf", [128, 256], "bfloat16"),
+    "pm":   ("sbuf", [128, 80], "bfloat16"),
+    "xs":   ("sbuf", [128, TOKS], "bfloat16"),
+    "gs":   ("sbuf", [128, TOKS], "bfloat16"),
+    "rr":   ("sbuf", [128, 128], "bfloat16"),
+    "sel":  ("sbuf", [128, NR * 128], "bfloat16"),
+    "mask": ("sbuf", [128, TOKS], "bfloat16"),
+    "gm":   ("sbuf", [128, TOKS], "bfloat16"),
+    "zero": ("sbuf", [128, HALF], "bfloat16"),
+    "hh":   ("sbuf", [128, NR * TOKS], "bfloat16"),
+    "hg":   ("sbuf", [128, NR * TOKS], "bfloat16"),
+    "ys":   ("sbuf", [128, TOKS], "bfloat16"),
+    "pgr":  ("psum", [128, 512], "float32"),
+    "pgb0": ("psum", [128, 512], "float32"),
+    "pgb1": ("psum", [128, 512], "float32"),
+    "pz0":  ("psum", [128, 512], "float32"),
+    "pz1":  ("psum", [128, 512], "float32"),
+    "py0":  ("psum", [128, 512], "float32"),
+    "py1":  ("psum", [128, 512], "float32"),
+}
+SEMAPHORES = (["lw", "lx", "lg", "pc", "msk", "gr", "gmd", "st", "ls", "rly", "pp", "yd0", "yd1", "cp0", "cp1"]
+              + ["wa%d" % e for e in range(NR)] + ["z%d" % k for k in range(NR)] + ["gb%d" % k for k in range(NR)]
+              + ["rl%d_%d" % (k, h) for k in range(NR) for h in range(2)]
+              + ["mu%d_%d" % (k, h) for k in range(NR) for h in range(2)])
+
+
+def _bits(m):
+    return bin(m).count("1")
+
+
+def _chip_cores(c0, topo):
+    return [c for c in range(NSIM) if topo.host(c) == topo.host(c0) and topo.chip(c) == topo.chip(c0)]
+
+
+def _plan(cores, topo):
+    n = len(cores)
+    cls = [[q for q in range(n) if q == r or topo.may_write(cores[r], cores[q])] for r in range(n)]
+    sends = []
+    for r in range(n):
+        c0 = cores[r]
+        helpers = [c for c in _chip_cores(c0, topo) if c != c0]
+        a = cls[r].index(r)
+        far = [d for d in range(n) if d not in cls[r]]
+        used = []
+        acts = []
+        nf = len(far)
+        for j in range(nf):
+            d = far[(j + a * (nf // 2 if nf > 2 else 1)) % nf]
+            want = (a + cls[d].index(d)) % 2
+            cand = [c for c in helpers if c not in used and topo.may_write(c, cores[d])]
+            pick = [c for c in cand if topo.die(c) == want] or cand
+            used.append(pick[0])
+            acts.append((pick[0], d))
+        near = [cls[r][(a + k) % len(cls[r])] for k in range(1, len(cls[r]))]
+        if len(near) >= 3:
+            d = near[0]
+            cand = [c for c in helpers if c not in used and topo.may_write(c, cores[d])]
+            pick = ([c for c in cand if topo.die(c) != topo.die(c0) and not any(topo.may_write(c, cores[q]) for q in far)]
+                    or [c for c in cand if topo.die(c) != topo.die(c0)] or cand)
+            used.append(pick[0])
+            acts.append((pick[0], d))
+            near = near[1:]
+        for d in near:
+            acts.append((None, d))
+        sends.append(acts)
+    return sends
+
+
+def _order(r, sends):
+    est = []
+    for s in range(len(sends)):
+        if s == r:
+            continue
+        nrel = len([1 for via, d in sends[s] if via is not None])
+        nd = 0
+        for j, (via, d) in enumerate(sends[s]):
+            if via is None:
+                nd += 1
+            if d == r:
+                est.append(((j + 1) + 2.5 if via is not None else nrel + 2 * nd, s))
+    return [r] + [s for _, s in sorted(est)]
+
+
+def _cover(d, n, w):
+    allowed = [d[t] >= n for t in range(w)]
+    unc = set(t for t in range(w) if d[t] == n)
+    out = []
+    while unc:
+        best = None
+        for s in sorted(unc):
+            for step in range(1, w - s + 1):
+                t, cnt, k, bl = s, 0, 0, None
+                while t < w and allowed[t]:
+                    k += 1
+                    if t in unc:
+                        cnt += 1
+                        bl = (cnt, k)
+                    t += step
+                if best is None or bl[0] > best[0]:
+                    best = (bl[0], s, step, bl[1])
+        _, s, step, k = best
+        out.append((s, step, k))
+        for j in range(k):
+            unc.discard(s + j * step)
+            allowed[s + j * step] = False
+    return out
+
+
+def _digit(route_t, i):
+    d = route_t[i] - i
+    return 3 - d if i == 2 else d
+
+
+def _sel_rows(e, i):
+    v = [0.0, 0.0, 0.0, 0.0]
+    k = e - i
+    if 0 <= k <= 3:
+        if i == 2:
+            k = 3 - k
+        v[k] = 1.0
+        if k + 1 <= 3:
+            v[k + 1] = -1.0
+    return v
+
+
+def _blocks(nh):
+    units = TOKS // 8
+    out, a = [], 0
+    for h in range(nh):
+        u = units // nh + (1 if h < units % nh else 0)
+        out.append((a, 8 * u))
+        a += 8 * u
+    return out
+
+
+def _fill(v, layers, sem):
+    n = 0
+    for layer in layers:
+        if n and layer:
+            v.wait_ge(sem, n)
+        for ap, val in layer:
+            v.memset(ap, val).then_inc(sem, 1)
+            n += 1
+    return n
+
+
+def _helper(g, core, T, topo, r, sends):
+    cores = T.cores
+    c0 = cores[r]
+    helpers = [c for c in _chip_cores(c0, topo) if c != c0]
+    a, w = _blocks(len(helpers))[helpers.index(core)]
+    route = T.tables["ROUTE"][r]
+    v = g.vector
+    layers = [[(T.pm[:, 0:w], 0.0)], [], [], [], []]
+    for i in range(3):
+        d = [_digit(route[a + t], i) for t in range(w)]
+        layers[1].append((T.pm[32 * i:32 * i + 1, 0:w], 1.0))
+        for lv in (1, 2, 3):
+            for s, step, k in _cover(d, lv, w):
+                layers[lv + 1].append((T.pm[32 * i:32 * i + lv + 1, s:s + (k - 1) * step + 1:step], 1.0))
+    np_ = _fill(v, layers, T.sem.pp)
+    peer = [q for q in cores if topo.may_write(core, q) and (topo.host(q), topo.chip(q)) != (topo.host(core), topo.chip(core))][0]
+    m = topo.mask(core, c0) & topo.mask(core, peer)
+    nls = 0
+    g.wait_ge(T.sem.pp, np_)
+    rid, pid = topo.addr(c0, core)
+    g.remote_dma(T.mask[:, a:a + w], T.pm[:, 0:w], T.sem.msk, T.sem.ls, pid, rid, m)
+    nls += _bits(m)
+    dsts = [d for via, d in sends[r] if via == core]
+    if dsts:
+        g.wait_ge(T.sem.rly, _bits(topo.mask(c0, core)))
+        for d in dsts:
+            rid, pid = topo.addr(cores[d], core)
+            m = topo.mask(core, cores[d])
+            g.remote_dma(T.wall[:, r * 256:(r + 1) * 256], T.rb[:, :], T.sem["wa%d" % r], T.sem.ls, pid, rid, m)
+            nls += _bits(m)
+    g.wait_ge(T.sem.ls, nls)
+
+
+def rank_program(g, core, T, topo):
+    cores = T.cores
+    sends = _plan(cores, topo)
+    rank = T.rank_of(core)
+    if rank is None:
+        for r in range(len(cores)):
+            if core in _chip_cores(cores[r], topo):
+                _helper(g, core, T, topo, r, sends)
+        return
+    r = rank
+    S = T.sem
+    v, pe = g.vector, g.tensor
+    own = T.wall[:, r * 256:(r + 1) * 256]
+    helpers = [c for c in _chip_cores(core, topo) if c != core]
+
+    g.sync.dma_start(T.wall[:, r * 256:r * 256 + 128], T.w1[:, :]).then_inc(S.lw, 16)
+    g.scalar.dma_start(T.wall[:, r * 256 + 128:r * 256 + 256], T.w2[:, :]).then_inc(S.lw, 16)
+    g.sync.dma_start(T.xs[:, :], T.x[:, :]).then_inc(S.lx, 16)
+    g.scalar.dma_start(T.gs[0:3, :], T.gate[:, :]).then_inc(S.lg, 16)
+
+    g.wait_ge(S.lw, 32)
+    nls = 0
+    for via, d in sends[r]:
+        if via is not None:
+            rid, pid = topo.addr(via, core)
+            m = topo.mask(core, via)
+            g.remote_dma(T.rb[:, :], own, S.rly, S.ls, pid, rid, m)
+        else:
+            rid, pid = topo.addr(cores[d], core)
+            m = topo.mask(core, cores[d])
+            g.remote_dma(own, own, S["wa%d" % r], S.ls, pid, rid, m)
+        nls += _bits(m)
+
+    layers = [[(T.zero[:, :], 0.0), (T.rr[0:3, :], 0.0), (T.sel[:, :], 0.0)], [], [], []]
+    for i in range(3):
+        layers[1].append((T.rr[0:i + 1, 32 * i:32 * i + 4], 1.0))
+        if i:
+            layers[2].append((T.rr[0:i, 32 * i:32 * i + 4], 0.0))
+    for e in range(NR):
+        for i in range(3):
+            rows = _sel_rows(e, i)
+            above, l = 0.0, 1
+            for j in (3, 2, 1, 0):
+                if rows[j] != above:
+                    layers[l].append((T.sel[32 * i:32 * i + j + 1, e * 128:(e + 1) * 128], rows[j]))
+                    l += 1
+                above = rows[j]
+    npc = _fill(v, layers, S.pc)
+
+    order = _order(r, sends)
+    pz = [T.pz0, T.pz1]
+    pgb = [T.pgb0, T.pgb1]
+    py = [T.py0, T.py1]
+    arrive = {}
+    for s in range(len(cores)):
+        for via, d in sends[s]:
+            if d == r:
+                arrive[s] = _bits(topo.mask(via if via is not None else cores[s], core))
+
+    def w1_of(e):
+        return T.wall[:, e * 256:e * 256 + 128]
+
+    def w2_of(e):
+        return T.wall[:, e * 256 + 128:e * 256 + 256]
+
+    def mm1(k):
+        pe.matmul(pz[k % 2][:, :], w1_of(order[k]), T.xs[:, :], True, True).then_inc(S["z%d" % k], 1)
+
+    def gbm(k):
+        e = order[k]
+        pe.matmul(pgb[k % 2][:, :], T.sel[:, e * 128:(e + 1) * 128], T.gm[:, :], True, True).then_inc(S["gb%d" % k], 1)
+
+    def mm2(k):
+        for h in range(2):
+            pe.wait_ge(S["mu%d_%d" % (k, h)], 1)
+            ins = pe.matmul(py[h][:, 0:HALF], w2_of(order[k]), T.hg[:, k * TOKS + h * HALF:k * TOKS + (h + 1) * HALF],
+                            k == 0, k == NR - 1)
+            if k == NR - 1:
+                ins.then_inc(S["yd%d" % h], 1)
+
+    pe.wait_ge(S.lw, 32)
+    pe.wait_ge(S.lx, 16)
+    mm1(0)
+    pe.wait_ge(S.pc, npc)
+    pe.wait_ge(S.lg, 16)
+    pe.matmul(T.pgr[:, :], T.rr[0:3, :], T.gs[0:3, :], True, True).then_inc(S.gr, 1)
+    pe.wait_ge(S.gmd, 1)
+    gbm(0)
+    gbm(1)
+    for k in range(1, NR):
+        pe.wait_ge(S["wa%d" % order[k]], arrive[order[k]])
+        if k >= 2:
+            pe.wait_ge(S["rl%d_0" % (k - 2)], 1)
+            pe.wait_ge(S["rl%d_1" % (k - 2)], 1)
+        mm1(k)
+        mm2(k - 1)
+        if k + 1 < NR:
+            gbm(k + 1)
+    mm2(NR - 1)
+
+    def relu(k):
+        v.wait_ge(S["z%d" % k], 1)
+        for h in range(2):
+            v.tensor_tensor(T.hh[:, k * TOKS + h * HALF:k * TOKS + (h + 1) * HALF], pz[k % 2][:, h * HALF:(h + 1) * HALF],
+                            T.zero[:, :], AluOpType.max).then_inc(S["rl%d_%d" % (k, h)], 1)
+
+    def gated(k):
+        v.wait_ge(S["gb%d" % k], 1)
+        for h in range(2):
+            v.wait_ge(S["rl%d_%d" % (k, h)], 1)
+            v.tensor_tensor(T.hg[:, k * TOKS + h * HALF:k * TOKS + (h + 1) * HALF],
+                            T.hh[:, k * TOKS + h * HALF:k * TOKS + (h + 1) * HALF],
+                            pgb[k % 2][:, h * HALF:(h + 1) * HALF], AluOpType.mult).then_inc(S["mu%d_%d" % (k, h)], 1)
+
+    v.wait_ge(S.pc, npc)
+    relu(0)
+    nmsk = 0
+    for c in helpers:
+        peer = [q for q in cores if topo.may_write(c, q) and (topo.host(q), topo.chip(q)) != (topo.host(c), topo.chip(c))][0]
+        nmsk += _bits(topo.mask(c, core) & topo.mask(c, peer))
+    v.wait_ge(S.msk, nmsk)
+    v.wait_ge(S.gr, 1)
+    v.tensor_tensor(T.gm[:, :], T.mask[:, :], T.pgr[:, :], AluOpType.mult).then_inc(S.gmd, 1)
+    gated(0)
+    for k in range(1, NR):
+        relu(k)
+        gated(k)
+    for h in range(2):
+        v.wait_ge(S["yd%d" % h], 1)
+        v.tensor_copy(T.ys[:, h * HALF:(h + 1) * HALF], py[h][:, 0:HALF]).then_inc(S["cp%d" % h], 1)
+
+    g.sync.wait_ge(S.cp0, 1)
+    g.sync.dma_start(T.y[:, 0:HALF], T.ys[:, 0:HALF]).then_inc(S.st, 16)
+    g.scalar.wait_ge(S.cp1, 1)
+    g.scalar.dma_start(T.y[:, HALF:TOKS], T.ys[:, HALF:TOKS]).then_inc(S.st, 16)
+
+    g.wait_ge(S.ls, nls)
+    g.wait_ge(S.st, 32)

@@ -1,18 +1,23 @@
+from concourse.bass import DstId, RemoteDMATransfer
 from concourse.mybir import dt, AluOpType
 
 NSIM = 256
 TOKS = 512
 HALF = 256
 NR = 6
+NFAR = 24
+DELTA = 20
+SELF = 7
+WMAX = 80
 
 SCRATCH = {
     "wall": ("sbuf", [128, NR * 256], "bfloat16"),
     "rb":   ("sbuf", [128, 256], "bfloat16"),
-    "pm":   ("sbuf", [128, 80], "bfloat16"),
+    "pm":   ("sbuf", [128, WMAX], "bfloat16"),
+    "sb":   ("sbuf", [128, 128], "bfloat16"),
     "xs":   ("sbuf", [128, TOKS], "bfloat16"),
     "gs":   ("sbuf", [128, TOKS], "bfloat16"),
-    "rr":   ("sbuf", [128, 128], "bfloat16"),
-    "sel":  ("sbuf", [128, NR * 128], "bfloat16"),
+    "sel":  ("sbuf", [128, (NR + 1) * 128], "bfloat16"),
     "mask": ("sbuf", [128, TOKS], "bfloat16"),
     "gm":   ("sbuf", [128, TOKS], "bfloat16"),
     "zero": ("sbuf", [128, HALF], "bfloat16"),
@@ -27,23 +32,34 @@ SCRATCH = {
     "py0":  ("psum", [128, 512], "float32"),
     "py1":  ("psum", [128, 512], "float32"),
 }
-SEMAPHORES = (["lw", "lx", "lg", "pc", "msk", "gr", "gmd", "st", "ls", "rly", "pp", "yd0", "yd1", "cp0", "cp1"]
+SEMAPHORES = (["lw", "lx", "lg", "pc", "msk", "sl", "gr", "gmd", "st", "ls", "rly", "pp", "pq", "yd0", "yd1", "cp0", "cp1"]
               + ["wa%d" % e for e in range(NR)] + ["z%d" % k for k in range(NR)] + ["gb%d" % k for k in range(NR)]
               + ["rl%d_%d" % (k, h) for k in range(NR) for h in range(2)]
               + ["mu%d_%d" % (k, h) for k in range(NR) for h in range(2)])
+
+_CACHE = {}
 
 
 def _bits(m):
     return bin(m).count("1")
 
 
+def _place(c, topo):
+    return (topo.host(c), topo.chip(c))
+
+
 def _chip_cores(c0, topo):
-    return [c for c in range(NSIM) if topo.host(c) == topo.host(c0) and topo.chip(c) == topo.chip(c0)]
+    return [c for c in range(NSIM) if _place(c, topo) == _place(c0, topo)]
+
+
+def _classes(cores, topo):
+    n = len(cores)
+    return [[q for q in range(n) if q == r or topo.may_write(cores[r], cores[q])] for r in range(n)]
 
 
 def _plan(cores, topo):
     n = len(cores)
-    cls = [[q for q in range(n) if q == r or topo.may_write(cores[r], cores[q])] for r in range(n)]
+    cls = _classes(cores, topo)
     sends = []
     for r in range(n):
         c0 = cores[r]
@@ -61,15 +77,12 @@ def _plan(cores, topo):
             used.append(pick[0])
             acts.append((pick[0], d))
         near = [cls[r][(a + k) % len(cls[r])] for k in range(1, len(cls[r]))]
-        if len(near) >= 3:
-            d = near[0]
+        for j, d in enumerate(near[:-1]):
             cand = [c for c in helpers if c not in used and topo.may_write(c, cores[d])]
-            pick = ([c for c in cand if topo.die(c) != topo.die(c0) and not any(topo.may_write(c, cores[q]) for q in far)]
-                    or [c for c in cand if topo.die(c) != topo.die(c0)] or cand)
+            pick = [c for c in cand if (topo.die(c) != topo.die(c0)) == (j % 2 == 0)] or cand
             used.append(pick[0])
             acts.append((pick[0], d))
-            near = near[1:]
-        for d in near:
+        for d in near[-1:]:
             acts.append((None, d))
         sends.append(acts)
     return sends
@@ -78,15 +91,9 @@ def _plan(cores, topo):
 def _order(r, sends):
     est = []
     for s in range(len(sends)):
-        if s == r:
-            continue
-        nrel = len([1 for via, d in sends[s] if via is not None])
-        nd = 0
         for j, (via, d) in enumerate(sends[s]):
-            if via is None:
-                nd += 1
             if d == r:
-                est.append(((j + 1) + 2.5 if via is not None else nrel + 2 * nd, s))
+                est.append((2 * (j + 1) + 2.5 if via is not None else 2, s))
     return [r] + [s for _, s in sorted(est)]
 
 
@@ -132,14 +139,65 @@ def _sel_rows(e, i):
     return v
 
 
-def _blocks(nh):
-    units = TOKS // 8
-    out, a = [], 0
-    for h in range(nh):
-        u = units // nh + (1 if h < units % nh else 0)
-        out.append((a, 8 * u))
-        a += 8 * u
-    return out
+def _fills(r, route, a, w):
+    key = ("f", r, a, w)
+    if key not in _CACHE:
+        lev = [[], [], []]
+        for i in range(3):
+            d = [_digit(route[a + t], i) for t in range(w)]
+            for lv in (1, 2, 3):
+                for s, step, k in _cover(d, lv, w):
+                    lev[lv - 1].append((i, s, step, k))
+        _CACHE[key] = lev
+    return _CACHE[key]
+
+
+def _try(r, route, kinds, c):
+    a, out = 0, []
+    for near in kinds:
+        budget = c - (SELF if near else DELTA) - 4
+        w = 0
+        while a + w + 2 <= TOKS and w + 2 <= WMAX and sum(len(l) for l in _fills(r, route, a, w + 2)) <= budget:
+            w += 2
+        out.append((a, w))
+        a += w
+    return out if a == TOKS else None
+
+
+def _painters(r, cores, topo):
+    key = ("p", r)
+    if key not in _CACHE:
+        c0 = cores[r]
+        out = [(c, True) for c in _chip_cores(c0, topo) if c != c0]
+        cl = _classes(cores, topo)[r]
+        busy = [_place(q, topo) for q in cores]
+        idle = []
+        for c in range(NSIM):
+            if (topo.same_plane(c, c0) and _place(c, topo) not in busy and _place(c, topo) not in idle
+                    and not any(topo.mates(c, q) for q in cores)):
+                idle.append(_place(c, topo))
+        mine = idle[cl.index(r)::len(cl)]
+        far = [c for c in range(NSIM) if _place(c, topo) in mine and topo.may_write(c, c0)]
+        _CACHE[key] = out + [(c, False) for c in far[:NFAR]]
+    return _CACHE[key]
+
+
+def _alloc(r, T, topo):
+    key = ("a", r)
+    if key not in _CACHE:
+        route = T.tables["ROUTE"][r]
+        ps = _painters(r, T.cores, topo)
+        kinds = [near for _, near in ps]
+        lo, hi = DELTA, 100
+        while lo < hi:
+            mid = (lo + hi) // 2
+            if _try(r, route, kinds, mid) is None:
+                lo = mid + 1
+            else:
+                hi = mid
+        blocks = _try(r, route, kinds, lo)
+        _CACHE[key] = dict((ps[j][0], blocks[j]) for j in range(len(ps)) if blocks[j][1] > 0)
+    return _CACHE[key]
 
 
 def _fill(v, layers, sem):
@@ -153,37 +211,66 @@ def _fill(v, layers, sem):
     return n
 
 
+def _small_mask(c, c0, cores, topo):
+    peer = [q for q in cores if topo.may_write(c, q) and _place(q, topo) != _place(c, topo)][0]
+    return topo.mask(c, c0) & topo.mask(c, peer)
+
+
 def _helper(g, core, T, topo, r, sends):
     cores = T.cores
     c0 = cores[r]
-    helpers = [c for c in _chip_cores(c0, topo) if c != c0]
-    a, w = _blocks(len(helpers))[helpers.index(core)]
-    route = T.tables["ROUTE"][r]
     v = g.vector
-    layers = [[(T.pm[:, 0:w], 0.0)], [], [], [], []]
-    for i in range(3):
-        d = [_digit(route[a + t], i) for t in range(w)]
-        layers[1].append((T.pm[32 * i:32 * i + 1, 0:w], 1.0))
-        for lv in (1, 2, 3):
-            for s, step, k in _cover(d, lv, w):
-                layers[lv + 1].append((T.pm[32 * i:32 * i + lv + 1, s:s + (k - 1) * step + 1:step], 1.0))
-    np_ = _fill(v, layers, T.sem.pp)
-    peer = [q for q in cores if topo.may_write(core, q) and (topo.host(q), topo.chip(q)) != (topo.host(core), topo.chip(core))][0]
-    m = topo.mask(core, c0) & topo.mask(core, peer)
     nls = 0
-    g.wait_ge(T.sem.pp, np_)
+    m = _small_mask(core, c0, cores, topo)
     rid, pid = topo.addr(c0, core)
-    g.remote_dma(T.mask[:, a:a + w], T.pm[:, 0:w], T.sem.msk, T.sem.ls, pid, rid, m)
-    nls += _bits(m)
-    dsts = [d for via, d in sends[r] if via == core]
-    if dsts:
-        g.wait_ge(T.sem.rly, _bits(topo.mask(c0, core)))
-        for d in dsts:
-            rid, pid = topo.addr(cores[d], core)
-            m = topo.mask(core, cores[d])
-            g.remote_dma(T.wall[:, r * 256:(r + 1) * 256], T.rb[:, :], T.sem["wa%d" % r], T.sem.ls, pid, rid, m)
-            nls += _bits(m)
-    g.wait_ge(T.sem.ls, nls)
+    helpers = [c for c in _chip_cores(c0, topo) if c != c0]
+    if core in helpers:
+        b = helpers.index(core)
+        layers = [[(T.sb[:, :], 0.0)], [], [], []]
+        for i in range(3):
+            if b < NR:
+                rows, above, l = _sel_rows(b, i), 0.0, 1
+                for j in (3, 2, 1, 0):
+                    if rows[j] != above:
+                        layers[l].append((T.sb[32 * i:32 * i + j + 1, :], rows[j]))
+                        l += 1
+                    above = rows[j]
+            else:
+                layers[1].append((T.sb[0:i + 1, 32 * i:32 * i + 4], 1.0))
+                if i:
+                    layers[2].append((T.sb[0:i, 32 * i:32 * i + 4], 0.0))
+        n = _fill(v, layers, T.sem.pq)
+        g.wait_ge(T.sem.pq, n)
+        g.remote_dma(T.sel[:, b * 128:(b + 1) * 128], T.sb[:, :], T.sem.sl, T.sem.ls, pid, rid, m)
+        nls += _bits(m)
+    al = _alloc(r, T, topo)
+    if core in al:
+        a, w = al[core]
+        lev = _fills(r, T.tables["ROUTE"][r], a, w)
+        layers = [[(T.pm[:, 0:w], 0.0)], [(T.pm[32 * i:32 * i + 1, 0:w], 1.0) for i in range(3)]]
+        for lv in (1, 2, 3):
+            layers.append([(T.pm[32 * i:32 * i + lv + 1, s:s + (k - 1) * step + 1:step], 1.0) for i, s, step, k in lev[lv - 1]])
+        n = _fill(v, layers, T.sem.pp)
+        g.wait_ge(T.sem.pp, n)
+        g.remote_dma(T.mask[:, a:a + w], T.pm[:, 0:w], T.sem.msk, T.sem.ls, pid, rid, m)
+        nls += _bits(m)
+    for d in [d for via, d in sends[r] if via == core]:
+        g.wait_ge(T.sem.rly, _bits(_relay_engines(c0, cores, sends[r], topo)))
+        rid, pid = topo.addr(cores[d], core)
+        m = topo.mask(core, cores[d])
+        g.remote_dma(T.wall[:, r * 256:(r + 1) * 256], T.rb[:, :], T.sem["wa%d" % r], T.sem.ls, pid, rid, m)
+        nls += _bits(m)
+    if nls:
+        g.wait_ge(T.sem.ls, nls)
+
+
+def _relay_engines(c0, cores, acts, topo):
+    m = 0
+    for via, d in acts:
+        if via is None:
+            m |= topo.mask(c0, cores[d])
+    on = topo.mask(c0, [via for via, d in acts if via is not None][0])
+    return on & ~m
 
 
 def rank_program(g, core, T, topo):
@@ -192,7 +279,7 @@ def rank_program(g, core, T, topo):
     rank = T.rank_of(core)
     if rank is None:
         for r in range(len(cores)):
-            if core in _chip_cores(cores[r], topo):
+            if core in [c for c, _ in _painters(r, cores, topo)]:
                 _helper(g, core, T, topo, r, sends)
         return
     r = rank
@@ -207,33 +294,24 @@ def rank_program(g, core, T, topo):
     g.scalar.dma_start(T.gs[0:3, :], T.gate[:, :]).then_inc(S.lg, 16)
 
     g.wait_ge(S.lw, 32)
-    nls = 0
+    trs, nls = [], 0
     for via, d in sends[r]:
-        if via is not None:
-            rid, pid = topo.addr(via, core)
-            m = topo.mask(core, via)
-            g.remote_dma(T.rb[:, :], own, S.rly, S.ls, pid, rid, m)
-        else:
+        if via is None:
             rid, pid = topo.addr(cores[d], core)
             m = topo.mask(core, cores[d])
-            g.remote_dma(own, own, S["wa%d" % r], S.ls, pid, rid, m)
-        nls += _bits(m)
-
-    layers = [[(T.zero[:, :], 0.0), (T.rr[0:3, :], 0.0), (T.sel[:, :], 0.0)], [], [], []]
-    for i in range(3):
-        layers[1].append((T.rr[0:i + 1, 32 * i:32 * i + 4], 1.0))
-        if i:
-            layers[2].append((T.rr[0:i, 32 * i:32 * i + 4], 0.0))
-    for e in range(NR):
-        for i in range(3):
-            rows = _sel_rows(e, i)
-            above, l = 0.0, 1
-            for j in (3, 2, 1, 0):
-                if rows[j] != above:
-                    layers[l].append((T.sel[32 * i:32 * i + j + 1, e * 128:(e + 1) * 128], rows[j]))
-                    l += 1
-                above = rows[j]
-    npc = _fill(v, layers, S.pc)
+            trs.append(RemoteDMATransfer(dst_ids=[DstId(rid=rid, pnc=pid)], dma_engine_mask=m, remote_sem=S["wa%d" % r],
+                                         srcs=[own], dsts=[own], alu_op=0))
+            nls += _bits(m)
+    vias = [via for via, d in sends[r] if via is not None]
+    ids = []
+    for via in vias:
+        rid, pid = topo.addr(via, core)
+        ids.append(DstId(rid=rid, pnc=pid))
+    m = _relay_engines(core, cores, sends[r], topo)
+    trs.append(RemoteDMATransfer(dst_ids=ids, dma_engine_mask=m, remote_sem=S.rly, srcs=[own],
+                                 dsts=[T.rb[:, :] for _ in vias], alu_op=0))
+    nls += _bits(m)
+    g.remote_dma_fused(trs, local_sem=S.ls)
 
     order = _order(r, sends)
     pz = [T.pz0, T.pz1]
@@ -269,21 +347,24 @@ def rank_program(g, core, T, topo):
     pe.wait_ge(S.lw, 32)
     pe.wait_ge(S.lx, 16)
     mm1(0)
-    pe.wait_ge(S.pc, npc)
+    pe.wait_ge(S.sl, sum(_bits(_small_mask(c, core, cores, topo)) for c in helpers))
     pe.wait_ge(S.lg, 16)
-    pe.matmul(T.pgr[:, :], T.rr[0:3, :], T.gs[0:3, :], True, True).then_inc(S.gr, 1)
+    pe.matmul(T.pgr[:, :], T.sel[0:3, NR * 128:(NR + 1) * 128], T.gs[0:3, :], True, True).then_inc(S.gr, 1)
     pe.wait_ge(S.gmd, 1)
     gbm(0)
     gbm(1)
-    for k in range(1, NR):
+    pe.wait_ge(S["wa%d" % order[1]], arrive[order[1]])
+    mm1(1)
+    for k in range(2, NR):
         pe.wait_ge(S["wa%d" % order[k]], arrive[order[k]])
-        if k >= 2:
-            pe.wait_ge(S["rl%d_0" % (k - 2)], 1)
-            pe.wait_ge(S["rl%d_1" % (k - 2)], 1)
+        pe.wait_ge(S["rl%d_0" % (k - 2)], 1)
+        pe.wait_ge(S["rl%d_1" % (k - 2)], 1)
         mm1(k)
-        mm2(k - 1)
-        if k + 1 < NR:
-            gbm(k + 1)
+        pe.wait_ge(S["mu%d_0" % (k - 2)], 1)
+        pe.wait_ge(S["mu%d_1" % (k - 2)], 1)
+        gbm(k)
+        mm2(k - 2)
+    mm2(NR - 2)
     mm2(NR - 1)
 
     def relu(k):
@@ -300,13 +381,10 @@ def rank_program(g, core, T, topo):
                             T.hh[:, k * TOKS + h * HALF:k * TOKS + (h + 1) * HALF],
                             pgb[k % 2][:, h * HALF:(h + 1) * HALF], AluOpType.mult).then_inc(S["mu%d_%d" % (k, h)], 1)
 
-    v.wait_ge(S.pc, npc)
+    v.memset(T.zero[:, :], 0.0).then_inc(S.pc, 1)
+    v.wait_ge(S.pc, 1)
     relu(0)
-    nmsk = 0
-    for c in helpers:
-        peer = [q for q in cores if topo.may_write(c, q) and (topo.host(q), topo.chip(q)) != (topo.host(c), topo.chip(c))][0]
-        nmsk += _bits(topo.mask(c, core) & topo.mask(c, peer))
-    v.wait_ge(S.msk, nmsk)
+    v.wait_ge(S.msk, sum(_bits(_small_mask(c, core, cores, topo)) for c in _alloc(r, T, topo)))
     v.wait_ge(S.gr, 1)
     v.tensor_tensor(T.gm[:, :], T.mask[:, :], T.pgr[:, :], AluOpType.mult).then_inc(S.gmd, 1)
     gated(0)

from concourse.bass import DstId, RemoteDMATransfer
from concourse.mybir import dt, AluOpType

NSIM = 256
TOKS = 512
HALF = 256
NR = 6
NFAR = 24
DELTA = 20
SELF = 7
WMAX = 80

SCRATCH = {
    "wall": ("sbuf", [128, NR * 256], "bfloat16"),
    "rb":   ("sbuf", [128, 256], "bfloat16"),
    "pm":   ("sbuf", [128, WMAX], "bfloat16"),
    "sb":   ("sbuf", [128, 128], "bfloat16"),
    "xs":   ("sbuf", [128, TOKS], "bfloat16"),
    "gs":   ("sbuf", [128, TOKS], "bfloat16"),
    "sel":  ("sbuf", [128, (NR + 1) * 128], "bfloat16"),
    "mask": ("sbuf", [128, TOKS], "bfloat16"),
    "gm":   ("sbuf", [128, TOKS], "bfloat16"),
    "zero": ("sbuf", [128, HALF], "bfloat16"),
    "hh":   ("sbuf", [128, NR * TOKS], "bfloat16"),
    "hg":   ("sbuf", [128, NR * TOKS], "bfloat16"),
    "ys":   ("sbuf", [128, TOKS], "bfloat16"),
    "pgr":  ("psum", [128, 512], "float32"),
    "pgb0": ("psum", [128, 512], "float32"),
    "pgb1": ("psum", [128, 512], "float32"),
    "pz0":  ("psum", [128, 512], "float32"),
    "pz1":  ("psum", [128, 512], "float32"),
    "py0":  ("psum", [128, 512], "float32"),
    "py1":  ("psum", [128, 512], "float32"),
}
SEMAPHORES = (["lw", "lx", "lg", "pc", "msk", "sl", "gr", "gmd", "st", "ls", "rly", "pp", "pq", "yd0", "yd1", "cp0", "cp1"]
              + ["wa%d" % e for e in range(NR)] + ["z%d" % k for k in range(NR)] + ["gb%d" % k for k in range(NR)]
              + ["rl%d_%d" % (k, h) for k in range(NR) for h in range(2)]
              + ["mu%d_%d" % (k, h) for k in range(NR) for h in range(2)])

_CACHE = {}


def _bits(m):
    return bin(m).count("1")


def _place(c, topo):
    return (topo.host(c), topo.chip(c))


def _chip_cores(c0, topo):
    return [c for c in range(NSIM) if _place(c, topo) == _place(c0, topo)]


def _classes(cores, topo):
    n = len(cores)
    return [[q for q in range(n) if q == r or topo.may_write(cores[r], cores[q])] for r in range(n)]


def _plan(cores, topo):
    n = len(cores)
    cls = _classes(cores, topo)
    sends = []
    for r in range(n):
        c0 = cores[r]
        helpers = [c for c in _chip_cores(c0, topo) if c != c0]
        a = cls[r].index(r)
        far = [d for d in range(n) if d not in cls[r]]
        used = []
        acts = []
        nf = len(far)
        for j in range(nf):
            d = far[(j + a * (nf // 2 if nf > 2 else 1)) % nf]
            want = (a + cls[d].index(d)) % 2
            cand = [c for c in helpers if c not in used and topo.may_write(c, cores[d])]
            pick = [c for c in cand if topo.die(c) == want] or cand
            used.append(pick[0])
            acts.append((pick[0], d))
        near = [cls[r][(a + k) % len(cls[r])] for k in range(1, len(cls[r]))]
        for j, d in enumerate(near[:-1]):
            cand = [c for c in helpers if c not in used and topo.may_write(c, cores[d])]
            pick = [c for c in cand if (topo.die(c) != topo.die(c0)) == (j % 2 == 0)] or cand
            used.append(pick[0])
            acts.append((pick[0], d))
        for d in near[-1:]:
            acts.append((None, d))
        sends.append(acts)
    return sends


def _order(r, sends):
    est = []
    for s in range(len(sends)):
        for j, (via, d) in enumerate(sends[s]):
            if d == r:
                est.append((2 * (j + 1) + 2.5 if via is not None else 2, s))
    return [r] + [s for _, s in sorted(est)]


def _cover(d, n, w):
    allowed = [d[t] >= n for t in range(w)]
    unc = set(t for t in range(w) if d[t] == n)
    out = []
    while unc:
        best = None
        for s in sorted(unc):
            for step in range(1, w - s + 1):
                t, cnt, k, bl = s, 0, 0, None
                while t < w and allowed[t]:
                    k += 1
                    if t in unc:
                        cnt += 1
                        bl = (cnt, k)
                    t += step
                if best is None or bl[0] > best[0]:
                    best = (bl[0], s, step, bl[1])
        _, s, step, k = best
        out.append((s, step, k))
        for j in range(k):
            unc.discard(s + j * step)
            allowed[s + j * step] = False
    return out


def _digit(route_t, i):
    d = route_t[i] - i
    return 3 - d if i == 2 else d


def _sel_rows(e, i):
    v = [0.0, 0.0, 0.0, 0.0]
    k = e - i
    if 0 <= k <= 3:
        if i == 2:
            k = 3 - k
        v[k] = 1.0
        if k + 1 <= 3:
            v[k + 1] = -1.0
    return v


def _fills(r, route, a, w):
    key = ("f", r, a, w)
    if key not in _CACHE:
        lev = [[], [], []]
        for i in range(3):
            d = [_digit(route[a + t], i) for t in range(w)]
            for lv in (1, 2, 3):
                for s, step, k in _cover(d, lv, w):
                    lev[lv - 1].append((i, s, step, k))
        _CACHE[key] = lev
    return _CACHE[key]


def _try(r, route, kinds, c):
    a, out = 0, []
    for near in kinds:
        budget = c - (SELF if near else DELTA) - 4
        w = 0
        while a + w + 2 <= TOKS and w + 2 <= WMAX and sum(len(l) for l in _fills(r, route, a, w + 2)) <= budget:
            w += 2
        out.append((a, w))
        a += w
    return out if a == TOKS else None


def _painters(r, cores, topo):
    key = ("p", r)
    if key not in _CACHE:
        c0 = cores[r]
        out = [(c, True) for c in _chip_cores(c0, topo) if c != c0]
        cl = _classes(cores, topo)[r]
        busy = [_place(q, topo) for q in cores]
        idle = []
        for c in range(NSIM):
            if (topo.same_plane(c, c0) and _place(c, topo) not in busy and _place(c, topo) not in idle
                    and not any(topo.mates(c, q) for q in cores)):
                idle.append(_place(c, topo))
        mine = idle[cl.index(r)::len(cl)]
        far = [c for c in range(NSIM) if _place(c, topo) in mine and topo.may_write(c, c0)]
        _CACHE[key] = out + [(c, False) for c in far[:NFAR]]
    return _CACHE[key]


def _alloc(r, T, topo):
    key = ("a", r)
    if key not in _CACHE:
        route = T.tables["ROUTE"][r]
        ps = _painters(r, T.cores, topo)
        kinds = [near for _, near in ps]
        lo, hi = DELTA, 100
        while lo < hi:
            mid = (lo + hi) // 2
            if _try(r, route, kinds, mid) is None:
                lo = mid + 1
            else:
                hi = mid
        blocks = _try(r, route, kinds, lo)
        _CACHE[key] = dict((ps[j][0], blocks[j]) for j in range(len(ps)) if blocks[j][1] > 0)
    return _CACHE[key]


def _fill(v, layers, sem):
    n = 0
    for layer in layers:
        if n and layer:
            v.wait_ge(sem, n)
        for ap, val in layer:
            v.memset(ap, val).then_inc(sem, 1)
            n += 1
    return n


def _small_mask(c, c0, cores, topo):
    peer = [q for q in cores if topo.may_write(c, q) and _place(q, topo) != _place(c, topo)][0]
    return topo.mask(c, c0) & topo.mask(c, peer)


def _helper(g, core, T, topo, r, sends):
    cores = T.cores
    c0 = cores[r]
    v = g.vector
    nls = 0
    m = _small_mask(core, c0, cores, topo)
    rid, pid = topo.addr(c0, core)
    helpers = [c for c in _chip_cores(c0, topo) if c != c0]
    if core in helpers:
        b = helpers.index(core)
        layers = [[(T.sb[:, :], 0.0)], [], [], []]
        for i in range(3):
            if b < NR:
                rows, above, l = _sel_rows(b, i), 0.0, 1
                for j in (3, 2, 1, 0):
                    if rows[j] != above:
                        layers[l].append((T.sb[32 * i:32 * i + j + 1, :], rows[j]))
                        l += 1
                    above = rows[j]
            else:
                layers[1].append((T.sb[0:i + 1, 32 * i:32 * i + 4], 1.0))
                if i:
                    layers[2].append((T.sb[0:i, 32 * i:32 * i + 4], 0.0))
        n = _fill(v, layers, T.sem.pq)
        g.wait_ge(T.sem.pq, n)
        g.remote_dma(T.sel[:, b * 128:(b + 1) * 128], T.sb[:, :], T.sem.sl, T.sem.ls, pid, rid, m)
        nls += _bits(m)
    al = _alloc(r, T, topo)
    if core in al:
        a, w = al[core]
        lev = _fills(r, T.tables["ROUTE"][r], a, w)
        layers = [[(T.pm[:, 0:w], 0.0)], [(T.pm[32 * i:32 * i + 1, 0:w], 1.0) for i in range(3)]]
        for lv in (1, 2, 3):
            layers.append([(T.pm[32 * i:32 * i + lv + 1, s:s + (k - 1) * step + 1:step], 1.0) for i, s, step, k in lev[lv - 1]])
        n = _fill(v, layers, T.sem.pp)
        g.wait_ge(T.sem.pp, n)
        g.remote_dma(T.mask[:, a:a + w], T.pm[:, 0:w], T.sem.msk, T.sem.ls, pid, rid, m)
        nls += _bits(m)
    for d in [d for via, d in sends[r] if via == core]:
        g.wait_ge(T.sem.rly, _bits(_relay_engines(c0, cores, sends[r], topo)))
        rid, pid = topo.addr(cores[d], core)
        m = topo.mask(core, cores[d])
        g.remote_dma(T.wall[:, r * 256:(r + 1) * 256], T.rb[:, :], T.sem["wa%d" % r], T.sem.ls, pid, rid, m)
        nls += _bits(m)
    if nls:
        g.wait_ge(T.sem.ls, nls)


def _relay_engines(c0, cores, acts, topo):
    m = 0
    for via, d in acts:
        if via is None:
            m |= topo.mask(c0, cores[d])
    on = topo.mask(c0, [via for via, d in acts if via is not None][0])
    return on & ~m


def rank_program(g, core, T, topo):
    cores = T.cores
    sends = _plan(cores, topo)
    rank = T.rank_of(core)
    if rank is None:
        for r in range(len(cores)):
            if core in [c for c, _ in _painters(r, cores, topo)]:
                _helper(g, core, T, topo, r, sends)
        return
    r = rank
    S = T.sem
    v, pe = g.vector, g.tensor
    own = T.wall[:, r * 256:(r + 1) * 256]
    helpers = [c for c in _chip_cores(core, topo) if c != core]

    g.sync.dma_start(T.wall[:, r * 256:r * 256 + 128], T.w1[:, :]).then_inc(S.lw, 16)
    g.scalar.dma_start(T.wall[:, r * 256 + 128:r * 256 + 256], T.w2[:, :]).then_inc(S.lw, 16)
    g.sync.dma_start(T.xs[:, :], T.x[:, :]).then_inc(S.lx, 16)
    g.scalar.dma_start(T.gs[0:3, :], T.gate[:, :]).then_inc(S.lg, 16)

    g.wait_ge(S.lw, 32)
    trs, nls = [], 0
    for via, d in sends[r]:
        if via is None:
            rid, pid = topo.addr(cores[d], core)
            m = topo.mask(core, cores[d])
            trs.append(RemoteDMATransfer(dst_ids=[DstId(rid=rid, pnc=pid)], dma_engine_mask=m, remote_sem=S["wa%d" % r],
                                         srcs=[own], dsts=[own], alu_op=0))
            nls += _bits(m)
    vias = [via for via, d in sends[r] if via is not None]
    ids = []
    for via in vias:
        rid, pid = topo.addr(via, core)
        ids.append(DstId(rid=rid, pnc=pid))
    m = _relay_engines(core, cores, sends[r], topo)
    trs.append(RemoteDMATransfer(dst_ids=ids, dma_engine_mask=m, remote_sem=S.rly, srcs=[own],
                                 dsts=[T.rb[:, :] for _ in vias], alu_op=0))
    nls += _bits(m)
    g.remote_dma_fused(trs, local_sem=S.ls)

    order = _order(r, sends)
    pz = [T.pz0, T.pz1]
    pgb = [T.pgb0, T.pgb1]
    py = [T.py0, T.py1]
    arrive = {}
    for s in range(len(cores)):
        for via, d in sends[s]:
            if d == r:
                arrive[s] = _bits(topo.mask(via if via is not None else cores[s], core))

    def w1_of(e):
        return T.wall[:, e * 256:e * 256 + 128]

    def w2_of(e):
        return T.wall[:, e * 256 + 128:e * 256 + 256]

    def mm1(k):
        pe.matmul(pz[k % 2][:, :], w1_of(order[k]), T.xs[:, :], True, True).then_inc(S["z%d" % k], 1)

    def gbm(k):
        e = order[k]
        pe.matmul(pgb[k % 2][:, :], T.sel[:, e * 128:(e + 1) * 128], T.gm[:, :], True, True).then_inc(S["gb%d" % k], 1)

    def mm2(k):
        for h in range(2):
            pe.wait_ge(S["mu%d_%d" % (k, h)], 1)
            ins = pe.matmul(py[h][:, 0:HALF], w2_of(order[k]), T.hg[:, k * TOKS + h * HALF:k * TOKS + (h + 1) * HALF],
                            k == 0, k == NR - 1)
            if k == NR - 1:
                ins.then_inc(S["yd%d" % h], 1)

    pe.wait_ge(S.lw, 32)
    pe.wait_ge(S.lx, 16)
    mm1(0)
    pe.wait_ge(S.sl, sum(_bits(_small_mask(c, core, cores, topo)) for c in helpers))
    pe.wait_ge(S.lg, 16)
    pe.matmul(T.pgr[:, :], T.sel[0:3, NR * 128:(NR + 1) * 128], T.gs[0:3, :], True, True).then_inc(S.gr, 1)
    pe.wait_ge(S.gmd, 1)
    gbm(0)
    gbm(1)
    pe.wait_ge(S["wa%d" % order[1]], arrive[order[1]])
    mm1(1)
    for k in range(2, NR):
        pe.wait_ge(S["wa%d" % order[k]], arrive[order[k]])
        pe.wait_ge(S["rl%d_0" % (k - 2)], 1)
        pe.wait_ge(S["rl%d_1" % (k - 2)], 1)
        mm1(k)
        pe.wait_ge(S["mu%d_0" % (k - 2)], 1)
        pe.wait_ge(S["mu%d_1" % (k - 2)], 1)
        gbm(k)
        mm2(k - 2)
    mm2(NR - 2)
    mm2(NR - 1)

    def relu(k):
        v.wait_ge(S["z%d" % k], 1)
        for h in range(2):
            v.tensor_tensor(T.hh[:, k * TOKS + h * HALF:k * TOKS + (h + 1) * HALF], pz[k % 2][:, h * HALF:(h + 1) * HALF],
                            T.zero[:, :], AluOpType.max).then_inc(S["rl%d_%d" % (k, h)], 1)

    def gated(k):
        v.wait_ge(S["gb%d" % k], 1)
        for h in range(2):
            v.wait_ge(S["rl%d_%d" % (k, h)], 1)
            v.tensor_tensor(T.hg[:, k * TOKS + h * HALF:k * TOKS + (h + 1) * HALF],
                            T.hh[:, k * TOKS + h * HALF:k * TOKS + (h + 1) * HALF],
                            pgb[k % 2][:, h * HALF:(h + 1) * HALF], AluOpType.mult).then_inc(S["mu%d_%d" % (k, h)], 1)

    v.memset(T.zero[:, :], 0.0).then_inc(S.pc, 1)
    v.wait_ge(S.pc, 1)
    relu(0)
    v.wait_ge(S.msk, sum(_bits(_small_mask(c, core, cores, topo)) for c in _alloc(r, T, topo)))
    v.wait_ge(S.gr, 1)
    v.tensor_tensor(T.gm[:, :], T.mask[:, :], T.pgr[:, :], AluOpType.mult).then_inc(S.gmd, 1)
    gated(0)
    for k in range(1, NR):
        relu(k)
        gated(k)
    for h in range(2):
        v.wait_ge(S["yd%d" % h], 1)
        v.tensor_copy(T.ys[:, h * HALF:(h + 1) * HALF], py[h][:, 0:HALF]).then_inc(S["cp%d" % h], 1)

    g.sync.wait_ge(S.cp0, 1)
    g.sync.dma_start(T.y[:, 0:HALF], T.ys[:, 0:HALF]).then_inc(S.st, 16)
    g.scalar.wait_ge(S.cp1, 1)
    g.scalar.dma_start(T.y[:, HALF:TOKS], T.ys[:, HALF:TOKS]).then_inc(S.st, 16)

    g.wait_ge(S.ls, nls)
    g.wait_ge(S.st, 32)
